import numpy as np, ml_dtypes
CORES = [16,17,18,19,32,33,34,35]
N = 8
BF = ml_dtypes.bfloat16
def f(rng, *shape):
    return (rng.standard_normal(shape, dtype=np.float32) * np.exp2(rng.integers(-2, 3, shape[:-1] + (1,)))).astype(BF)
def wide(rng, *shape):
    v = f(rng, *shape).astype(np.float32); k = shape[:-2] + (1, shape[-1])
    return (v * np.exp2(rng.integers(-6, 7, k)) * (rng.random(k) > 0.0625)).astype(BF)
def gentries(a):
    return np.ascontiguousarray(a.reshape(8, 16, -1).transpose(0, 2, 1)).reshape(8, -1)
def gtable(e):
    e = np.asarray(e); return np.ascontiguousarray(e.reshape(8, -1, 16).transpose(0, 2, 1)).reshape(128, -1).astype(np.int32)
E, M, CAPP, R = 2048, 2688, 64, 3
GX, GY, GZ = 16, 16, 8
def mesh(rng):
    return np.stack([np.stack([rng.permutation(M)[:E] for c in range(8)]) for r in range(N)])
def counts(rng, lo):
    n = np.triu(rng.integers(lo, CAPP + 1, (N, N)), 1); r = int(rng.integers(0, N - 1)); n[r, int(rng.integers(r + 1, N))] = CAPP; return n
def several(rng, k):
    return [sorted(rng.choice(N, int(j), replace=False).tolist()) for j in rng.integers(3, N + 1, k)]
def shares(rng, num, sets, pool):
    h = np.tile(M + np.arange(CAPP), (N, 8, 1)); left = np.array(num); at = [0] * N; same = []
    free = {(r, q): rng.permutation(CAPP).tolist() for r in range(N) for q in range(r + 1, N)}
    def join(S):
        n = [int(pool[r][at[r]]) for r in S]
        for i, r in enumerate(S):
            at[r] += 1
            for j in range(i + 1, len(S)):
                q = S[j]; k = free[r, q].pop(); h[r, q, k] = n[i]; h[q, r, k] = n[j]; left[r, q] -= 1
            if i: same.append((S[0], n[0], r, n[i]))
    for S in sets:
        if all(left[S[i], S[j]] > 0 for i in range(len(S)) for j in range(i + 1, len(S))): join(S)
    for r in range(N):
        for q in range(r + 1, N):
            for i in range(int(left[r, q])): join([r, q])
    return h, same
def make(rng, c, hs, u, st):
    h, same = hs; w = ((0.5 + rng.random((N, 1, M))) * 0.125).astype(BF); u = np.array(u)
    for r, n, q, m in same:
        u[q, :, m] = u[r, :, n]; w[q, 0, m] = w[r, 0, n]
    return {"u": u, "w": w, "ke": rng.standard_normal((N, 8, 8)).astype(BF), "st": st.astype(BF), "conn": np.stack([gtable(a) for a in c]), "share": np.stack([gtable(a) for a in h])}
def setup_inputs(rng):
    c = mesh(rng); hs = shares(rng, counts(rng, CAPP // 2), several(rng, CAPP // 2), [rng.permutation(M) for r in range(N)])
    return make(rng, c, hs, f(rng, N, 16, M), 0.5 + rng.random((N, 1, E)))
def setup_inputs_grid(rng):
    e = np.arange(E); x, y, z = e % GX, e // GX % GY, e // (GX * GY)
    c = np.stack([((z + (k >> 2)) * (GY + 1) + y + (k >> 1 & 1)) * (GX + 1) + x + (k & 1) for k in range(8)])
    n = np.arange((GX + 1) * (GY + 1) * (GZ + 1)); x, y, z = n % (GX + 1), n // (GX + 1) % (GY + 1), n // ((GX + 1) * (GY + 1))
    n = n[(x == 0) | (x == GX) | (y == 0) | (y == GY) | (z == 0) | (z == GZ)]
    b = rng.integers(0, M - (GX + 1) * (GY + 1) * (GZ + 1) + 1, N)
    hs = shares(rng, counts(rng, 1), several(rng, CAPP // 4), [b[r] + rng.permutation(n) for r in range(N)])
    return make(rng, np.stack([c + b[r] for r in range(N)]), hs, f(rng, N, 16, M), 0.5 + rng.random((N, 1, E)))
def setup_inputs_all(rng):
    hs = shares(rng, np.triu(np.full((N, N), CAPP), 1), [list(range(N))] * CAPP, [rng.permutation(M) for r in range(N)])
    return make(rng, mesh(rng), hs, f(rng, N, 16, M), 0.5 + rng.random((N, 1, E)))
def setup_inputs_few(rng):
    n = np.zeros((N, N), np.int64)
    for q in range(1, N): n[q - 1, q] = rng.integers(0, 4)
    r = int(rng.integers(0, N - 1)); q = int(rng.integers(r + 1, N)); n[r, q] = CAPP
    inner = np.arange(1, M - 1); pool = [np.concatenate([[0, M - 1], rng.permutation(inner)]) for k in range(N)]
    c = np.zeros((N, 8, E), np.int64)
    for k in range(N):
        for a in range(8): c[k, a] = np.concatenate([[M - 1 if a % 2 else 0], rng.permutation(inner)[:E - 2], [0 if a % 2 else M - 1]])
    k = (r, q)[int(rng.integers(0, 2))]; c[k] = c[k, :1]
    return make(rng, c, shares(rng, n, [], pool), f(rng, N, 16, M), 0.5 + rng.random((N, 1, E)))
def setup_inputs_spread(rng):
    c = mesh(rng); hs = shares(rng, counts(rng, CAPP // 4), several(rng, CAPP), [rng.permutation(M) for r in range(N)])
    return make(rng, c, hs, wide(rng, N, 16, M), np.exp2(rng.integers(-2, 3, (N, 1, E))) * (rng.random((N, 1, E)) > 0.0625))
def check_inputs(d):
    bad = []; c = np.stack([gentries(a) for a in d["conn"]]).astype(np.int64); h = np.stack([gentries(a) for a in d["share"]]).astype(np.int64)
    if not all(np.isfinite(d[k].astype(np.float32)).all() for k in ("u", "w", "ke", "st")): bad.append("finite")
    if c.min() < 0 or c.max() >= M: bad.append("conn_in_range")
    t = np.sort(c, -1)
    if (t[..., 1:] == t[..., :-1]).any(): bad.append("a_node_is_corner_c_of_one_element_at_most")
    used = (h >= 0) & (h < M)
    if not (used | (h == M + np.arange(CAPP))).all(): return bad + ["share_in_range"]
    t = np.sort(h, -1)
    if (t[..., 1:] == t[..., :-1]).any(): return bad + ["a_node_stands_once_in_a_pairs_slots"]
    if used[:, N:].any() or any(used[r, r].any() for r in range(N)): return bad + ["own_and_unused_groups_empty"]
    if not (used[:, :N] == used[:, :N].transpose(1, 0, 2)).all(): return bad + ["slots_in_use_on_both_sides"]
    cp = np.full((N, M, N), -1, np.int64); alike = True
    for r in range(N):
        cp[r, :, r] = np.arange(M)
        for q in range(N):
            if q != r:
                k = used[r, q]; a, b = h[r, q][k], h[q, r][k]; cp[r, a, q] = b
                alike = alike and bool((d["u"][r][:, a] == d["u"][q][:, b]).all() and (d["w"][r][:, a] == d["w"][q][:, b]).all())
    if not alike: bad.append("copies_alike")
    if not all((cp[r, h[r, q][used[r, q]]] == cp[q, h[q, r][used[q, r]]]).all() for r in range(N) for q in range(N) if q != r): bad.append("all_copies_listed")
    return bad
def reference(u, w, ke, st, conn, share):
    c = [gentries(a) for a in conn]; h = [gentries(a) for a in share]
    x = u.astype(np.float64); wt = w.astype(np.float64); km = ke.astype(np.float64); sf = st.astype(np.float64)
    for t in range(R):
        p = np.zeros((N, 16, M + CAPP), np.float64)
        for r in range(N):
            v = np.einsum('ab,lbe->lae', km[r], x[r][:, c[r]]) * sf[r]
            for a in range(8): p[r][:, c[r][a]] += v[:, a]
        z = np.array(p)
        for r in range(N):
            for q in range(N):
                if q != r: z[r][:, h[r][q]] += p[q][:, h[q][r]]
        x = x - wt * z[:, :, :M]
    return {"y": x.astype(np.float32)}

@@ -1,0 +1,358 @@
+from concourse.bass import DstId, RemoteDMATransfer
+from concourse.mybir import AluOpType, ActivationFunctionType
+
+E, M, CAPP, R, N = 2048, 2688, 64, 3, 8
+MC = (M + CAPP) // 16
+ME = 16 * MC
+XW = M + 8 * CAPP
+UW = 256
+BW = 448
+F32, BF, I32, U16 = "float32", "bfloat16", "int32", "uint16"
+
+SCRATCH = {
+    "bCI": ("sbuf", [128, 132], I32), "bC1": ("sbuf", [128, 132], I32), "bC2": ("sbuf", [128, 132], I32),
+    "bC3": ("sbuf", [128, 132], I32), "bCPF": ("sbuf", [128, 132], F32), "bC16": ("sbuf", [128, 128], U16),
+    "bCP16": ("sbuf", [128, 132], U16),
+    "bIP": ("sbuf", [128, 1], I32), "bAI": ("sbuf", [128, 8], I32), "bAF": ("sbuf", [128, 8], F32),
+    "bK": ("sbuf", [128, 4], F32), "bIMOD": ("sbuf", [128, 128], F32), "bICOL": ("sbuf", [128, 32], F32),
+    "bISB": ("sbuf", [128, 128], F32), "bSB": ("sbuf", [128, 128], BF), "bYB": ("sbuf", [128, 128], BF),
+    "bB": ("sbuf", [128, 128], F32), "bB2": ("sbuf", [128, 128], F32), "bMN": ("sbuf", [128, 32], F32),
+    "bMX": ("sbuf", [128, 32], F32), "bSHW": ("sbuf", [128, 32], F32), "bRX": ("sbuf", [128, 32], F32),
+    "bRN": ("sbuf", [128, 32], F32), "bNLX": ("sbuf", [128, 32], U16), "bNLN": ("sbuf", [128, 32], U16),
+    "bLM": ("sbuf", [128, 240], F32), "bEX": ("sbuf", [128, 1024], F32),
+    "bKEI": ("sbuf", [128, 8], BF), "bKEF": ("sbuf", [128, 128], F32), "bKEB": ("sbuf", [128, 128], BF),
+    "bON": ("sbuf", [128, 128], BF), "bWR": ("sbuf", [128, M], BF), "bSTR": ("sbuf", [128, E], BF),
+    "bU": ("sbuf", [128, M], BF), "bW": ("sbuf", [128, M], BF), "bWG": ("sbuf", [128, E], F32),
+    "bS": ("sbuf", [128, E], F32), "bG0": ("sbuf", [128, E], BF), "bG": ("sbuf", [128, E], F32),
+    "bV": ("sbuf", [128, E + 16], F32), "bWS": ("sbuf", [128, 512], F32), "bW2": ("sbuf", [128, M], F32),
+    "bX": ("sbuf", [128, XW], F32), "bEI": ("sbuf", [128, E], F32), "bINV": ("sbuf", [128, ME], F32),
+    "bISH": ("sbuf", [128, ME], F32), "bPOS": ("sbuf", [128, ME], F32),
+    "bBS": ("sbuf", [128, 64], F32), "bVAL": ("sbuf", [128, 64], F32),
+    "bLSR": ("sbuf", [128, 512], F32), "bDR": ("sbuf", [128, 512], F32), "bNR": ("sbuf", [128, 512], F32),
+    "bLST": ("sbuf", [128, 32], F32), "bDT": ("sbuf", [128, 32], F32), "bNT": ("sbuf", [128, 32], F32),
+    "bLS16": ("sbuf", [128, 32], U16), "bD16": ("sbuf", [128, 32], U16), "bN16": ("sbuf", [128, 32], U16),
+    "bIT": ("sbuf", [128, MC], F32), "bI16": ("sbuf", [128, MC], U16),
+    "bPT": ("sbuf", [128, MC], F32), "bPL": ("sbuf", [128, 22], F32), "bPL16": ("sbuf", [128, 22], U16),
+    "bE1": ("sbuf", [128, E], F32), "bE2": ("sbuf", [128, E], F32), "bCT": ("sbuf", [128, 128], F32),
+    "bCT16": ("sbuf", [128, 128], U16),
+    "bSD0": ("sbuf", [128, 64], F32), "bSD1": ("sbuf", [128, 64], F32), "bSD2": ("sbuf", [128, 64], F32),
+    "bR0": ("sbuf", [128, 64], F32), "bR1": ("sbuf", [128, 64], F32), "bR2": ("sbuf", [128, 64], F32),
+    "bEW": ("sbuf", [128, 528], F32), "bWT": ("sbuf", [128, 512], F32), "bTM": ("sbuf", [128, 512], F32),
+    "bTT": ("sbuf", [128, 512], F32), "bYG": ("sbuf", [128, 336], F32),
+    "P0": ("psum", [128, 512], F32), "P1": ("psum", [128, 512], F32), "P2": ("psum", [128, 512], F32),
+    "P3": ("psum", [128, 512], F32), "P4": ("psum", [128, 512], F32), "P5": ("psum", [128, 512], F32),
+    "P6": ("psum", [128, 512], F32), "P7": ("psum", [128, 512], F32),
+}
+SEMAPHORES = ["kV", "kS", "kP", "kG", "loc", "arr0", "arr1", "arr2", "dconn", "dshare", "dke", "dw", "dst", "du",
+              "dinv", "dls", "dd", "dn", "dct", "dpt", "dpl", "dy"]
+A = AluOpType
+AF = ActivationFunctionType
+
+
+def rank_program(g, core, T, topo):
+    rank = T.rank_of(core)
+    if rank is None:
+        return
+    eng = {"V": g.vector, "S": g.scalar, "P": g.tensor, "G": g, "Y": g.sync}
+    count, know, clock = {}, {q: {} for q in eng}, {}
+    wr, rd = {}, {}
+
+    def over(lst, a, b):
+        return [e for e in lst if e[0] < b and a < e[1]]
+
+    def need(q, r, w):
+        own, out = "k" + q, {}
+        for n, a, b in r:
+            for e in over(wr.get(n, []), a, b):
+                out[e[2]] = max(out.get(e[2], 0), e[3])
+        for n, a, b in w:
+            for e in over(wr.get(n, []), a, b):
+                if not (e[2] == own and n[0] == "P"):
+                    out[e[2]] = max(out.get(e[2], 0), e[3])
+            for e in over(rd.get(n, []), a, b):
+                if e[2] != own:
+                    out[e[2]] = max(out.get(e[2], 0), e[3])
+        return out
+
+    def wait(q, deps):
+        k = know[q]
+        for s in sorted(deps, key=lambda s: -len(clock.get((s, deps[s]), {}))):
+            v = deps[s]
+            if k.get(s, 0) < v:
+                eng[q].wait_ge(T.sem[s], v)
+                for s2, v2 in clock.get((s, v), {}).items():
+                    k[s2] = max(k.get(s2, 0), v2)
+                k[s] = max(k.get(s, 0), v)
+
+    def note(q, s, v, r, w):
+        c = dict(know[q])
+        c[s] = max(c.get(s, 0), v)
+        clock[(s, v)] = c
+        for n, a, b in w:
+            wr[n] = [e for e in wr.get(n, []) if not (a <= e[0] and e[1] <= b)] + [(a, b, s, v)]
+            rd[n] = [e for e in rd.get(n, []) if not (a <= e[0] and e[1] <= b)]
+        for n, a, b in r:
+            rd[n] = rd.get(n, []) + [(a, b, s, v)]
+
+    def bank(regs):
+        return [(n, 0, 512) if n[0] == "P" else (n, a, b) for n, a, b in regs]
+
+    def op(q, fn, r, w):
+        r, w = bank(r), bank(w)
+        w = w + [x for x in r if x[0][0] == "P"]
+        r2 = [x for x in r if not (x[0][0] == "P" and q == "P")]
+        wait(q, need(q, r2, w))
+        s = "k" + q
+        count[s] = count.get(s, 0) + 1
+        fn(eng[q]).then_inc(T.sem[s], 1)
+        note(q, s, count[s], [x for x in r if x[0][0] != "P"], w)
+
+    def dma(parts, s, r, w):
+        qs = []
+        for q, o, i in parts:
+            if q not in qs:
+                qs.append(q)
+                wait(q, need(q, r, w))
+            eng[q].dma_start(out=o, in_=i).then_inc(T.sem[s], 16)
+            count[s] = count.get(s, 0) + 16
+        note(qs[0], s, count[s], r, w)
+
+    def gather(q, dst, a, n, win, wn, off, c0):
+        o, i = T[dst][:, a:a + n], T[win][:, 0:wn].indirect(T[off][:, c0:c0 + n // 16])
+        r = [(win, 0, wn), (off, c0, c0 + n // 16)]
+        if q == "V":
+            op("V", lambda e: e.tensor_copy(out=o, in_=i), r, [(dst, a, a + n)])
+        else:
+            op("S", lambda e: e.activation(out=o, in_=i, func=AF.Copy), r, [(dst, a, a + n)])
+
+    def copy(q, dst, a, src, b, n, rows=128, scale=1.0):
+        o, i = T[dst][0:rows, a:a + n], T[src][0:rows, b:b + n]
+        if q == "V":
+            op("V", lambda e: e.tensor_copy(out=o, in_=i), [(src, b, b + n)], [(dst, a, a + n)])
+        else:
+            op("S", lambda e: e.activation(out=o, in_=i, func=AF.Copy, scale=scale), [(src, b, b + n)], [(dst, a, a + n)])
+
+    def ts(dst, a, src, b, n, s1, s2, op0, op1=None, r=(), rows=128):
+        o, i = T[dst][0:rows, a:a + n], T[src][0:rows, b:b + n]
+        if op1 is None:
+            f = lambda e: e.tensor_scalar(out=o, in0=i, scalar1=s1, scalar2=None, op0=op0)
+        else:
+            f = lambda e: e.tensor_scalar(out=o, in0=i, scalar1=s1, scalar2=s2, op0=op0, op1=op1)
+        op("V", f, [(src, b, b + n)] + list(r), [(dst, a, a + n)])
+
+    def tt(dst, a, s0, b, s1, c, n, o):
+        x, y, z = T[dst][:, a:a + n], T[s0][:, b:b + n], T[s1][:, c:c + n]
+        op("V", lambda e: e.tensor_tensor(out=x, in0=y, in1=z, op=o), [(s0, b, b + n), (s1, c, c + n)], [(dst, a, a + n)])
+
+    def fill(dst, a, n, val):
+        op("V", lambda e: e.memset(T[dst][:, a:a + n], val), [], [(dst, a, a + n)])
+
+    def mm(dst, a, n, lh, la, m, rh, ra, start=True, stop=True, rows=128):
+        o, l, x = T[dst][0:m, a:a + n], T[lh][0:rows, la:la + m], T[rh][0:rows, ra:ra + n]
+        op("P", lambda e: e.matmul(o, l, x, start, stop), [(lh, la, la + m), (rh, ra, ra + n)], [(dst, a, a + n)])
+
+    def iota(dst, a, n, pat, base, cm, rows=128, flag=True):
+        o = T[dst][0:rows, a:a + n]
+        if flag:
+            f = lambda e: e.iota(o, pat, base, cm, allow_small_or_imprecise_dtypes=True)
+        else:
+            f = lambda e: e.iota(o, pat, base, cm)
+        op("G", f, [], [(dst, a, a + n)])
+
+    dma([("Y", T.bCI[:, 0:128], T.conn[:, :])], "dconn", [], [("bCI", 0, 128)])
+    dma([("Y", T.bCI[:, 128:132], T.share[:, :])], "dshare", [], [("bCI", 128, 132)])
+    dma([("Y", T.bWR[0:1, :], T.w[:, :])], "dw", [], [("bWR", 0, M)])
+    dma([("Y", T.bKEI[0:8, :], T.ke[:, :])], "dke", [], [("bKEI", 0, 8)])
+    dma([("Y", T.bSTR[0:1, :], T.st[:, :])], "dst", [], [("bSTR", 0, E)])
+    dma([("YS"[k % 2], T.bU[16 * k:16 * k + 16, :], T.u[:, :]) for k in range(8)], "du", [], [("bU", 0, M)])
+    iota("bIP", 0, 1, [[0, 1]], 0, 1, flag=False)
+    iota("bIMOD", 0, 128, [[0, 8], [1, 16]], 0, 0)
+    iota("bICOL", 0, 32, [[1, 8], [0, 4]], 0, 0)
+    iota("bISB", 0, 128, [[1, 8], [0, 16]], 0, -1)
+    iota("bEI", 0, 512, [[1, 512]], 0, 0)
+    iota("bINV", 1600, ME - 1600, [[0, ME - 1600]], E, 0)
+    iota("bBS", 0, 32, [[256, 2], [64, 4], [2, 4]], 0, 0)
+    iota("bBS", 32, 32, [[256, 2], [64, 4], [2, 4]], 1, 0)
+    iota("bISH", 0, ME, [[0, ME]], 512, 0)
+    iota("bPOS", 0, ME, [[1, 16], [16, MC]], 0, 0)
+
+    fill("bON", 0, 128, 1.0)
+    for c, (o0, a0, o1, a1) in enumerate([(A.logical_shift_right, 4, A.bitwise_and, 1), (A.bitwise_and, 3, None, 0),
+                                          (A.logical_shift_right, 2, A.bitwise_and, 3), (A.logical_shift_right, 5, None, 0),
+                                          (A.bitwise_and, 15, None, 0), (A.logical_shift_right, 4, None, 0)]):
+        ts("bAI", c, "bIP", 0, 1, a0, a1, o0, o1)
+    copy("V", "bAF", 0, "bAI", 0, 6)
+    ts("bK", 0, "bAF", 0, 1, 4.0, T.bAF[:, 1:2], A.mult, A.add, r=[("bAF", 1, 2)])
+    ts("bK", 1, "bAF", 2, 1, 4.0, T.bAF[:, 3:4], A.mult, A.add, r=[("bAF", 3, 4)])
+    ts("bSB", 0, "bISB", 0, 128, 0.0, None, A.is_equal)
+    fill("bINV", 0, 1600, float(E))
+    ts("bB", 0, "bIMOD", 0, 128, T.bAF[:, 4:5], None, A.is_equal, r=[("bAF", 4, 5)])
+    for n in (512, 1024):
+        o, i, b = T.bEI[:, n:2 * n], T.bEI[:, 0:n], float(n)
+        op("S", lambda e: e.activation(out=o, in_=i, func=AF.Copy, bias=b), [("bEI", 0, n)], [("bEI", n, 2 * n)])
+    copy("V", "bC16", 0, "bCI", 0, 128)
+    ts("bC1", 0, "bCI", 0, 132, 15, None, A.bitwise_and)
+    ts("bC2", 0, "bCI", 0, 132, 4, None, A.logical_shift_right)
+    ts("bC3", 0, "bC1", 0, 132, float(MC), None, A.mult)
+    tt("bCPF", 0, "bC3", 0, "bC2", 0, 132, A.add)
+    copy("V", "bCP16", 0, "bCPF", 0, 132)
+    o = T.bINV[:, 0:ME].indirect(T.bCP16[:, 0:128])
+    op("V", lambda e: e.tensor_copy(out=o, in_=T.bEI[:, :]), [("bEI", 0, E), ("bCP16", 0, 128)], [("bINV", 0, ME)])
+    dma([("Y", T.bIT[:, :], T.bINV[0:128:16, :])], "dinv", [("bINV", 0, ME)], [("bIT", 0, MC)])
+    for k in range(6):
+        mm("P%d" % k, 0, BW, "bON", 0, 128, "bWR", BW * k, rows=1)
+        copy("S", "bW", BW * k, "P%d" % k, 0, BW, scale=-1.0)
+    mm("P6", 0, 128, "bKEI", 0, 8, "bSB", 0, rows=8)
+    copy("S", "bYB", 0, "P6", 0, 128, rows=8)
+    mm("P7", 0, 128, "bSB", 0, 128, "bYB", 0, rows=8)
+    for a, b, n in ((0, 128, 4), (4, 128, 4)):
+        copy("S", "bSHW", a, "bCPF", b, n)
+    copy("S", "bSHW", 8, "bSHW", 0, 8)
+    copy("S", "bSHW", 16, "bSHW", 0, 16)
+    for k in range(4):
+        mm("P%d" % k, 0, 512, "bON", 0, 128, "bSTR", 512 * k, rows=1)
+        gather("S", "bWG", 512 * k, 512, "bW", M, "bC16", 32 * k)
+    tt("bKEB", 0, "P7", 0, "bB", 0, 128, A.mult)
+    tt("bKEF", 0, "P7", 0, "bB", 0, 128, A.mult)
+    for k in range(4):
+        gather("S", "bG0", 512 * k, 512, "bU", M, "bC16", 32 * k)
+    ts("bMX", 0, "bICOL", 0, 32, T.bK[:, 0:1], None, A.is_equal, r=[("bK", 0, 1)])
+    ts("bB2", 0, "bIMOD", 0, 128, T.bK[:, 1:2], None, A.is_equal, r=[("bK", 1, 2)])
+    tt("bRX", 0, "bSHW", 0, "bMX", 0, 32, A.mult)
+    mm("P6", 0, 32, "bB2", 0, 128, "bRX", 0)
+    tt("bS", 0, "bWG", 0, "P0", 0, 512, A.mult)
+    copy("V", "bNLX", 0, "P6", 0, 32)
+    gather("S", "bLSR", 0, 512, "bINV", ME, "bNLX", 0)
+    dma([("Y", T.bLST[:, :], T.bLSR[0:128:16, :])], "dls", [("bLSR", 0, 512)], [("bLST", 0, 32)])
+    fill("bV", E, 16, 0.0)
+    for k in range(1, 4):
+        tt("bS", 512 * k, "bWG", 512 * k, "P%d" % k, 0, 512, A.mult)
+    for k in range(4):
+        mm("P%d" % (4 + k), 0, 512, "bKEB", 0, 128, "bG0", 512 * k)
+    for k in range(4):
+        tt("bV", 512 * k, "P%d" % (4 + k), 0, "bS", 512 * k, 512, A.mult)
+    fill("bLM", 0, 240, 0.0)
+    copy("V", "bLM", 112, "bB", 0, 16)
+    copy("V", "bLS16", 0, "bLST", 0, 32)
+
+    others = [q for q in range(N) if q != rank]
+    off = [q for q in others if topo.chip(T.cores[q]) != topo.chip(core)]
+    on = [q for q in others if q not in off]
+    eoff = topo.engines(core, T.cores[off[0]])
+    eon = [e for e in topo.engines(core, T.cores[on[0]]) if e not in eoff]
+    per = 2
+    lanes = {q: eoff[per * k:per * k + per] for k, q in enumerate(off)}
+    lanes.update({q: eon[per * k:per * k + per] for k, q in enumerate(on)})
+
+    def send(t):
+        wait("G", need("G", [("bSD%d" % t, 0, 64)], []))
+        tr = []
+        for q in off + on:
+            rid, pid, _ = topo.addr(T.cores[q])
+            tr.append(RemoteDMATransfer(dst_ids=[DstId(rid=rid, pnc=pid)], dma_engine_mask=sum(1 << e for e in lanes[q]),
+                                        remote_sem=T.sem["arr%d" % t], src=T["bSD%d" % t][:, 8 * q:8 * q + 8],
+                                        dst=T["bR%d" % t][:, 8 * rank:8 * rank + 8]))
+        g.remote_dma_fused(tr, local_sem=T.sem["loc"])
+        count["loc"] = count.get("loc", 0) + per * len(tr)
+        s = "arr%d" % t
+        count[s] = per * len(tr)
+        for q in others:
+            wr["bR%d" % t] = wr.get("bR%d" % t, []) + [(8 * q, 8 * q + 8, s, count[s])]
+
+    XS = M
+    for t in range(R):
+        src, win = ("bX", XW) if t else ("bU", M)
+        if t:
+            banks = [4, 5, 6, 7, 2, 3, 0, 1]
+            for k in range(8):
+                gather("V" if k in (0, 2) else "S", "bG", UW * k, UW, "bX", XW, "bCT16", 16 * k)
+                if k == 5 and t == 1:
+                    for h in range(2):
+                        copy("S", "bTT", 256 * h, "P%d" % h, 0, 256)
+            if t == 2:
+                for h in range(2):
+                    tt("bTT", 256 * h, "P%d" % h, 0, "bTT", 256 * h, 256, A.add)
+            for k in range(8):
+                p = "P%d" % banks[k]
+                mm(p, 0, UW, "bKEF", 0, 128, "bG", UW * k)
+                tt("bV", UW * k, p, 0, "bS", UW * k, UW, A.mult)
+        gather("S", "bWS", 0, 256, "bV", E + 16, "bLS16", 0)
+        gather("V", "bWS", 256, 256, "bV", E + 16, "bLS16", 16)
+        for s in range(8):
+            mm("P6", 0, 64, "bLM", 112 - 16 * s, 128, "bWS", 64 * s, start=s == 0, stop=s == 7)
+        if t == 0:
+            copy("V", "bI16", 0, "bIT", 0, MC)
+            for k in range(R):
+                fill("bR%d" % k, 8 * rank, 8, 0.0)
+            fill("bEW", 512, 16, 0.0)
+            ts("bMN", 0, "bICOL", 0, 32, T.bAF[:, 5:6], None, A.is_equal, r=[("bAF", 5, 6)])
+            tt("bRN", 0, "bSHW", 0, "bMN", 0, 32, A.mult)
+            ts("bK", 2, "bAF", 5, 1, 8.0, None, A.mult)
+            ts("bVAL", 0, "bBS", 0, 64, T.bK[:, 2:3], None, A.add, r=[("bK", 2, 3)])
+            oo = T.bISH[:, 0:ME].indirect(T.bCP16[:, 128:132])
+            op("V", lambda e: e.tensor_copy(out=oo, in_=T.bVAL[:, :]), [("bVAL", 0, 64), ("bCP16", 128, 132)], [("bISH", 0, ME)])
+        gather("S", "bW2", 0, BW, "bV", E + 16, "bI16", 0)
+        copy("S", "bSD%d" % t, 0, "P6", 0, 64)
+        send(t)
+        order = [0, 4, 5, 1, 2, 3]
+        for k in order[1:]:
+            gather("V" if k > 3 else "S", "bW2", BW * k, BW, "bV", E + 16, "bI16", 28 * k)
+        for k in order:
+            mm("P%d" % k, 0, BW, "bB", 0, 128, "bW2", BW * k)
+        if t == 0:
+            mm("P7", 0, 32, "bB", 0, 128, "bRN", 0)
+            copy("V", "bNLN", 0, "P7", 0, 32)
+            gather("S", "bDR", 0, 512, "bISH", ME, "bNLX", 0)
+            dma([("Y", T.bDT[:, :], T.bDR[0:128:16, :])], "dd", [("bDR", 0, 512)], [("bDT", 0, 32)])
+            gather("S", "bNR", 0, 512, "bPOS", ME, "bNLX", 0)
+            dma([("Y", T.bNT[:, :], T.bNR[0:128:16, :])], "dn", [("bNR", 0, 512)], [("bNT", 0, 32)])
+            for q in others:
+                oq = T.bPOS[:, 0:ME].indirect(T.bNLN[:, 4 * q:4 * q + 4])
+                op("V", lambda e: e.tensor_scalar(out=oq, in0=T.bBS[:, :], scalar1=1.0, scalar2=float(XS + 8 * q), op0=A.mult, op1=A.add),
+                   [("bBS", 0, 64), ("bNLN", 4 * q, 4 * q + 4)], [("bPOS", 0, ME)])
+            for s in range(8):
+                oe, se = T.bEX[:, 128 * s:128 * s + 128], T.bMN[:, 4 * s:4 * s + 1]
+                op("S", lambda e: e.activation(out=oe, in_=T.bB[:, :], func=AF.Copy, scale=se), [("bB", 0, 128), ("bMN", 4 * s, 4 * s + 1)], [("bEX", 128 * s, 128 * s + 128)])
+            gather("S", "bE1", 0, 1024, "bPOS", ME, "bCP16", 0)
+            gather("V", "bE1", 1024, 1024, "bPOS", ME, "bCP16", 64)
+            for i in range(16):
+                for q, h in (("S", 0), ("V", 1)):
+                    o2, i2 = T.bE2[:, 128 * i + 64 * h:128 * i + 64 * h + 64], T.bE1[:, 1024 * h + i:1024 * h + 1024:16]
+                    if q == "S":
+                        f = lambda e: e.activation(out=o2, in_=i2, func=AF.Copy)
+                    else:
+                        f = lambda e: e.tensor_copy(out=o2, in_=i2)
+                    op(q, f, [("bE1", 1024 * h, 1024 * h + 1024)], [("bE2", 128 * i + 64 * h, 128 * i + 64 * h + 64)])
+            dma([("Y", T.bCT[:, :], T.bE2[0:128:16, :])], "dct", [("bE2", 0, E)], [("bCT", 0, 128)])
+            dma([("Y", T.bPT[:, :], T.bPOS[0:128:16, :])], "dpt", [("bPOS", 0, ME)], [("bPT", 0, MC)])
+            dma([("Y", T.bPL[16 * k:16 * k + 16, 0:21], T.bPT[16 * k:16 * k + 16, 21 * k:21 * k + 21]) for k in range(8)],
+                "dpl", [("bPT", 0, MC)], [("bPL", 0, 21)])
+        for k in order:
+            tt("bX", BW * k, "P%d" % k, 0, "bX" if t else "bU", BW * k, BW, A.add)
+        if t == 0:
+            ts("bN16", 0, "bNT", 0, 32, float(M - 1), None, A.min)
+            copy("V", "bD16", 0, "bDT", 0, 32)
+            gather("S", "bTM", 0, 256, "bX", M, "bN16", 0)
+            gather("V", "bTM", 256, 256, "bX", M, "bN16", 16)
+        else:
+            ix = T.bX[:, 0:M].indirect(T.bN16[:, 0:32])
+            op("V", lambda e: e.tensor_tensor(out=T.bTM[:, :], in0=ix, in1=T.bTT[:, :], op=A.add),
+               [("bX", 0, M), ("bN16", 0, 32), ("bTT", 0, 512)], [("bTM", 0, 512)])
+        for s in range(8):
+            mm("P%d" % (7 - s // 4), 64 * (s % 4), 64, "bEX", 128 * s, 128, "bR%d" % t, 0)
+        copy("S", "bEW", 0, "P7", 0, 256)
+        copy("V", "bEW", 256, "P6", 0, 256)
+        gather("S", "bWT", 0, 256, "bEW", 528, "bD16", 0)
+        gather("V", "bWT", 256, 256, "bEW", 528, "bD16", 16)
+        for h in range(2):
+            mm("P%d" % h, 0, 256, "bB", 0, 128, "bWT", 256 * h)
+        for h in range(2):
+            tt("bX", XS + 256 * h, "P%d" % h, 0, "bTM", 256 * h, 256, A.add)
+        if t == 0:
+            copy("V", "bCT16", 0, "bCT", 0, 128)
+            copy("V", "bPL16", 0, "bPL", 0, 21)
+    gather("S", "bYG", 0, 160, "bX", XW, "bPL16", 0)
+    gather("V", "bYG", 160, 176, "bX", XW, "bPL16", 10)
+    dma([("YS"[k % 2], T.y[:, 336 * k:336 * k + 336], T.bYG[16 * k:16 * k + 16, :]) for k in range(8)], "dy", [("bYG", 0, 336)], [])
+    for s in sorted(count):
+        g.wait_ge(T.sem[s], count[s])

@@ -4,45 +4,34 @@ from concourse.mybir import AluOpType, ActivationFunctionType
 E, M, CAPP, R, N = 2048, 2688, 64, 3, 8
 MC = (M + CAPP) // 16
 ME = 16 * MC
-XW = M + 8 * CAPP
-UW = 256
+XS = M
+XW = M + N * CAPP
 BW = 448
+NF = 1752
 F32, BF, I32, U16 = "float32", "bfloat16", "int32", "uint16"
 
+
+def sb(n, d=F32):
+    return ("sbuf", [128, n], d)
+
+
 SCRATCH = {
-    "bCI": ("sbuf", [128, 132], I32), "bC1": ("sbuf", [128, 132], I32), "bC2": ("sbuf", [128, 132], I32),
-    "bC3": ("sbuf", [128, 132], I32), "bCPF": ("sbuf", [128, 132], F32), "bC16": ("sbuf", [128, 128], U16),
-    "bCP16": ("sbuf", [128, 132], U16),
-    "bIP": ("sbuf", [128, 1], I32), "bAI": ("sbuf", [128, 8], I32), "bAF": ("sbuf", [128, 8], F32),
-    "bK": ("sbuf", [128, 4], F32), "bIMOD": ("sbuf", [128, 128], F32), "bICOL": ("sbuf", [128, 32], F32),
-    "bISB": ("sbuf", [128, 128], F32), "bSB": ("sbuf", [128, 128], BF), "bYB": ("sbuf", [128, 128], BF),
-    "bB": ("sbuf", [128, 128], F32), "bB2": ("sbuf", [128, 128], F32), "bMN": ("sbuf", [128, 32], F32),
-    "bMX": ("sbuf", [128, 32], F32), "bSHW": ("sbuf", [128, 32], F32), "bRX": ("sbuf", [128, 32], F32),
-    "bRN": ("sbuf", [128, 32], F32), "bNLX": ("sbuf", [128, 32], U16), "bNLN": ("sbuf", [128, 32], U16),
-    "bLM": ("sbuf", [128, 240], F32), "bEX": ("sbuf", [128, 1024], F32),
-    "bKEI": ("sbuf", [128, 8], BF), "bKEF": ("sbuf", [128, 128], F32), "bKEB": ("sbuf", [128, 128], BF),
-    "bON": ("sbuf", [128, 128], BF), "bWR": ("sbuf", [128, M], BF), "bSTR": ("sbuf", [128, E], BF),
-    "bU": ("sbuf", [128, M], BF), "bW": ("sbuf", [128, M], BF), "bWG": ("sbuf", [128, E], F32),
-    "bS": ("sbuf", [128, E], F32), "bG0": ("sbuf", [128, E], BF), "bG": ("sbuf", [128, E], F32),
-    "bV": ("sbuf", [128, E + 16], F32), "bWS": ("sbuf", [128, 512], F32), "bW2": ("sbuf", [128, M], F32),
-    "bX": ("sbuf", [128, XW], F32), "bEI": ("sbuf", [128, E], F32), "bINV": ("sbuf", [128, ME], F32),
-    "bISH": ("sbuf", [128, ME], F32), "bPOS": ("sbuf", [128, ME], F32),
-    "bBS": ("sbuf", [128, 64], F32), "bVAL": ("sbuf", [128, 64], F32),
-    "bLSR": ("sbuf", [128, 512], F32), "bDR": ("sbuf", [128, 512], F32), "bNR": ("sbuf", [128, 512], F32),
-    "bLST": ("sbuf", [128, 32], F32), "bDT": ("sbuf", [128, 32], F32), "bNT": ("sbuf", [128, 32], F32),
-    "bLS16": ("sbuf", [128, 32], U16), "bD16": ("sbuf", [128, 32], U16), "bN16": ("sbuf", [128, 32], U16),
-    "bIT": ("sbuf", [128, MC], F32), "bI16": ("sbuf", [128, MC], U16),
-    "bPT": ("sbuf", [128, MC], F32), "bPL": ("sbuf", [128, 22], F32), "bPL16": ("sbuf", [128, 22], U16),
-    "bE1": ("sbuf", [128, E], F32), "bE2": ("sbuf", [128, E], F32), "bCT": ("sbuf", [128, 128], F32),
-    "bCT16": ("sbuf", [128, 128], U16),
-    "bSD0": ("sbuf", [128, 64], F32), "bSD1": ("sbuf", [128, 64], F32), "bSD2": ("sbuf", [128, 64], F32),
-    "bR0": ("sbuf", [128, 64], F32), "bR1": ("sbuf", [128, 64], F32), "bR2": ("sbuf", [128, 64], F32),
-    "bEW": ("sbuf", [128, 528], F32), "bWT": ("sbuf", [128, 512], F32), "bTM": ("sbuf", [128, 512], F32),
-    "bTT": ("sbuf", [128, 512], F32), "bYG": ("sbuf", [128, 336], F32),
-    "P0": ("psum", [128, 512], F32), "P1": ("psum", [128, 512], F32), "P2": ("psum", [128, 512], F32),
-    "P3": ("psum", [128, 512], F32), "P4": ("psum", [128, 512], F32), "P5": ("psum", [128, 512], F32),
-    "P6": ("psum", [128, 512], F32), "P7": ("psum", [128, 512], F32),
+    "bCI": sb(132, I32), "bC1": sb(132, I32), "bC2": sb(132, I32), "bC3": sb(132, I32), "bCPF": sb(132),
+    "bC16": sb(128, U16), "bCP16": sb(132, U16),
+    "bIP": sb(1, I32), "bAI": sb(8, I32), "bAF": sb(8), "bK": sb(4), "bIMOD": sb(128), "bICOL": sb(32),
+    "bJ": sb(128, BF), "bSB": sb(128, BF), "bYB": sb(128, BF), "bB": sb(128), "bB2": sb(128), "bMN": sb(32), "bMX": sb(32),
+    "bSHW": sb(32), "bRX": sb(32), "bRN": sb(32), "bNLX": sb(32, U16), "bNLN": sb(32, U16), "bLM": sb(240), "bEX": sb(1024),
+    "bKEI": sb(8, BF), "bKEF": sb(128), "bKEB": sb(128, BF), "bON": sb(128, BF), "bWR": sb(M, BF), "bSTR": sb(E, BF),
+    "bU": sb(M, BF), "bW": sb(M, BF), "bWG": sb(E), "bS": sb(E),
+    "bG0": sb(E, BF), "bG": sb(E), "bV": sb(E + 16), "bWS": sb(512), "bW2": sb(M), "bX": sb(XW),
+    "bSD0": sb(64), "bSD1": sb(64), "bSD2": sb(64), "bR0": sb(64), "bR1": sb(64), "bR2": sb(64),
+    "bEW": sb(528), "bWT": sb(512), "bYG": sb(336),
+    "bEI": sb(E), "bINV": sb(ME), "bISH": sb(ME), "bPOS": sb(ME), "bBS": sb(64), "bVAL": sb(64),
+    "bLSR": sb(512), "bDR": sb(512), "bNR": sb(512), "bLST": sb(32), "bDT": sb(32), "bNT": sb(32),
+    "bLS16": sb(32, U16), "bD16": sb(32, U16), "bN16": sb(32, U16), "bIT": sb(MC), "bI16": sb(MC, U16),
+    "bPT": sb(MC), "bPL": sb(22), "bPL16": sb(22, U16), "bE1": sb(E), "bE2": sb(E), "bCT": sb(128), "bCT16": sb(128, U16),
 }
+SCRATCH.update({"P%d" % k: ("psum", [128, 512], F32) for k in range(8)})
 SEMAPHORES = ["kV", "kS", "kP", "kG", "loc", "arr0", "arr1", "arr2", "dconn", "dshare", "dke", "dw", "dst", "du",
               "dinv", "dls", "dd", "dn", "dct", "dpt", "dpl", "dy"]
 A = AluOpType
@@ -159,49 +148,62 @@ def rank_program(g, core, T, topo):
             f = lambda e: e.iota(o, pat, base, cm)
         op("G", f, [], [(dst, a, a + n)])
 
+    def select(dst, rows, src, pat):
+        o, i = T[dst][0:rows, 0:128], T[src][0:rows, 0:128]
+        op("G", lambda e: e.affine_select(o, i, pat, A.is_equal, 0.0, 0, -1), [(src, 0, 128)], [(dst, 0, 128)])
+
     dma([("Y", T.bCI[:, 0:128], T.conn[:, :])], "dconn", [], [("bCI", 0, 128)])
     dma([("Y", T.bCI[:, 128:132], T.share[:, :])], "dshare", [], [("bCI", 128, 132)])
     dma([("Y", T.bWR[0:1, :], T.w[:, :])], "dw", [], [("bWR", 0, M)])
     dma([("Y", T.bKEI[0:8, :], T.ke[:, :])], "dke", [], [("bKEI", 0, 8)])
     dma([("Y", T.bSTR[0:1, :], T.st[:, :])], "dst", [], [("bSTR", 0, E)])
     dma([("YS"[k % 2], T.bU[16 * k:16 * k + 16, :], T.u[:, :]) for k in range(8)], "du", [], [("bU", 0, M)])
+    fill("bON", 0, 128, 1.0)
     iota("bIP", 0, 1, [[0, 1]], 0, 1, flag=False)
-    iota("bIMOD", 0, 128, [[0, 8], [1, 16]], 0, 0)
+    iota("bEI", 0, 256, [[1, 256]], 0, 0)
     iota("bICOL", 0, 32, [[1, 8], [0, 4]], 0, 0)
-    iota("bISB", 0, 128, [[1, 8], [0, 16]], 0, -1)
-    iota("bEI", 0, 512, [[1, 512]], 0, 0)
-    iota("bINV", 1600, ME - 1600, [[0, ME - 1600]], E, 0)
+    iota("bIMOD", 0, 128, [[0, 8], [1, 16]], 0, 0)
+    iota("bINV", NF, ME - NF, [[0, ME - NF]], E, 0)
+    select("bJ", 16, "bON", [[0, 8], [1, 16]])
+    select("bSB", 8, "bON", [[1, 8], [0, 16]])
+    iota("bV", E, 16, [[0, 16]], 0, 0)
+    iota("bEW", 512, 16, [[0, 16]], 0, 0)
+    iota("bLM", 0, 240, [[0, 240]], 0, 0)
+    for k in range(R):
+        iota("bR%d" % k, 8 * rank, 8, [[0, 8]], 0, 0)
+    iota("bPOS", 0, ME, [[1, 16], [16, MC]], 0, 0)
     iota("bBS", 0, 32, [[256, 2], [64, 4], [2, 4]], 0, 0)
     iota("bBS", 32, 32, [[256, 2], [64, 4], [2, 4]], 1, 0)
     iota("bISH", 0, ME, [[0, ME]], 512, 0)
-    iota("bPOS", 0, ME, [[1, 16], [16, MC]], 0, 0)
 
-    fill("bON", 0, 128, 1.0)
+    fill("bINV", 0, NF, float(E))
     for c, (o0, a0, o1, a1) in enumerate([(A.logical_shift_right, 4, A.bitwise_and, 1), (A.bitwise_and, 3, None, 0),
                                           (A.logical_shift_right, 2, A.bitwise_and, 3), (A.logical_shift_right, 5, None, 0),
-                                          (A.bitwise_and, 15, None, 0), (A.logical_shift_right, 4, None, 0)]):
+                                          (A.logical_shift_right, 4, None, 0)]):
         ts("bAI", c, "bIP", 0, 1, a0, a1, o0, o1)
-    copy("V", "bAF", 0, "bAI", 0, 6)
+    copy("V", "bAF", 0, "bAI", 0, 5)
     ts("bK", 0, "bAF", 0, 1, 4.0, T.bAF[:, 1:2], A.mult, A.add, r=[("bAF", 1, 2)])
     ts("bK", 1, "bAF", 2, 1, 4.0, T.bAF[:, 3:4], A.mult, A.add, r=[("bAF", 3, 4)])
-    ts("bSB", 0, "bISB", 0, 128, 0.0, None, A.is_equal)
-    fill("bINV", 0, 1600, float(E))
-    ts("bB", 0, "bIMOD", 0, 128, T.bAF[:, 4:5], None, A.is_equal, r=[("bAF", 4, 5)])
-    for n in (512, 1024):
+    ts("bMX", 0, "bICOL", 0, 32, T.bK[:, 0:1], None, A.is_equal, r=[("bK", 0, 1)])
+    ts("bMN", 0, "bICOL", 0, 32, T.bAF[:, 4:5], None, A.is_equal, r=[("bAF", 4, 5)])
+    ts("bB2", 0, "bIMOD", 0, 128, T.bK[:, 1:2], None, A.is_equal, r=[("bK", 1, 2)])
+    for n in (256, 512, 1024):
         o, i, b = T.bEI[:, n:2 * n], T.bEI[:, 0:n], float(n)
         op("S", lambda e: e.activation(out=o, in_=i, func=AF.Copy, bias=b), [("bEI", 0, n)], [("bEI", n, 2 * n)])
-    copy("V", "bC16", 0, "bCI", 0, 128)
     ts("bC1", 0, "bCI", 0, 132, 15, None, A.bitwise_and)
     ts("bC2", 0, "bCI", 0, 132, 4, None, A.logical_shift_right)
     ts("bC3", 0, "bC1", 0, 132, float(MC), None, A.mult)
     tt("bCPF", 0, "bC3", 0, "bC2", 0, 132, A.add)
     copy("V", "bCP16", 0, "bCPF", 0, 132)
-    o = T.bINV[:, 0:ME].indirect(T.bCP16[:, 0:128])
-    op("V", lambda e: e.tensor_copy(out=o, in_=T.bEI[:, :]), [("bEI", 0, E), ("bCP16", 0, 128)], [("bINV", 0, ME)])
+    copy("V", "bC16", 0, "bCI", 0, 128)
+    oi = T.bINV[:, 0:ME].indirect(T.bCP16[:, 0:128])
+    op("V", lambda e: e.tensor_copy(out=oi, in_=T.bEI[:, :]), [("bEI", 0, E), ("bCP16", 0, 128)], [("bINV", 0, ME)])
     dma([("Y", T.bIT[:, :], T.bINV[0:128:16, :])], "dinv", [("bINV", 0, ME)], [("bIT", 0, MC)])
     for k in range(6):
         mm("P%d" % k, 0, BW, "bON", 0, 128, "bWR", BW * k, rows=1)
         copy("S", "bW", BW * k, "P%d" % k, 0, BW, scale=-1.0)
+    mm("P7", 0, 128, "bJ", 0, 128, "bJ", 0, rows=16)
+    copy("S", "bB", 0, "P7", 0, 128)
     mm("P6", 0, 128, "bKEI", 0, 8, "bSB", 0, rows=8)
     copy("S", "bYB", 0, "P6", 0, 128, rows=8)
     mm("P7", 0, 128, "bSB", 0, 128, "bYB", 0, rows=8)
@@ -212,28 +214,34 @@ def rank_program(g, core, T, topo):
     for k in range(4):
         mm("P%d" % k, 0, 512, "bON", 0, 128, "bSTR", 512 * k, rows=1)
         gather("S", "bWG", 512 * k, 512, "bW", M, "bC16", 32 * k)
-    tt("bKEB", 0, "P7", 0, "bB", 0, 128, A.mult)
-    tt("bKEF", 0, "P7", 0, "bB", 0, 128, A.mult)
-    for k in range(4):
-        gather("S", "bG0", 512 * k, 512, "bU", M, "bC16", 32 * k)
-    ts("bMX", 0, "bICOL", 0, 32, T.bK[:, 0:1], None, A.is_equal, r=[("bK", 0, 1)])
-    ts("bB2", 0, "bIMOD", 0, 128, T.bK[:, 1:2], None, A.is_equal, r=[("bK", 1, 2)])
     tt("bRX", 0, "bSHW", 0, "bMX", 0, 32, A.mult)
     mm("P6", 0, 32, "bB2", 0, 128, "bRX", 0)
-    tt("bS", 0, "bWG", 0, "P0", 0, 512, A.mult)
+    tt("bKEB", 0, "P7", 0, "bB", 0, 128, A.mult)
+    tt("bRN", 0, "bSHW", 0, "bMN", 0, 32, A.mult)
+    for k in range(3):
+        gather("S", "bG0", 512 * k, 512, "bU", M, "bC16", 32 * k)
     copy("V", "bNLX", 0, "P6", 0, 32)
+    mm("P6", 0, 32, "bB", 0, 128, "bRN", 0)
     gather("S", "bLSR", 0, 512, "bINV", ME, "bNLX", 0)
     dma([("Y", T.bLST[:, :], T.bLSR[0:128:16, :])], "dls", [("bLSR", 0, 512)], [("bLST", 0, 32)])
-    fill("bV", E, 16, 0.0)
-    for k in range(1, 4):
+    gather("S", "bG0", 1536, 512, "bU", M, "bC16", 96)
+    for k in range(4):
         tt("bS", 512 * k, "bWG", 512 * k, "P%d" % k, 0, 512, A.mult)
+        if k == 0:
+            copy("V", "bNLN", 0, "P6", 0, 32)
     for k in range(4):
         mm("P%d" % (4 + k), 0, 512, "bKEB", 0, 128, "bG0", 512 * k)
     for k in range(4):
         tt("bV", 512 * k, "P%d" % (4 + k), 0, "bS", 512 * k, 512, A.mult)
-    fill("bLM", 0, 240, 0.0)
-    copy("V", "bLM", 112, "bB", 0, 16)
     copy("V", "bLS16", 0, "bLST", 0, 32)
+    copy("S", "bLM", 112, "bB", 0, 16)
+    gather("S", "bNR", 0, 512, "bPOS", ME, "bNLX", 0)
+    dma([("Y", T.bNT[:, :], T.bNR[0:128:16, :])], "dn", [("bNR", 0, 512)], [("bNT", 0, 32)])
+    for s in range(8):
+        oe, se = T.bEX[:, 128 * s:128 * s + 128], T.bMN[:, 4 * s:4 * s + 1]
+        op("S", lambda e: e.activation(out=oe, in_=T.bB[:, :], func=AF.Copy, scale=se),
+           [("bB", 0, 128), ("bMN", 4 * s, 4 * s + 1)], [("bEX", 128 * s, 128 * s + 128)])
+    copy("S", "bKEF", 0, "bKEB", 0, 128)
 
     others = [q for q in range(N) if q != rank]
     off = [q for q in others if topo.chip(T.cores[q]) != topo.chip(core)]
@@ -259,60 +267,36 @@ def rank_program(g, core, T, topo):
         for q in others:
             wr["bR%d" % t] = wr.get("bR%d" % t, []) + [(8 * q, 8 * q + 8, s, count[s])]
 
-    XS = M
+    def own_slots():
+        for h in range(4):
+            mm("P%d" % h, 0, 128, "bB", 0, 128, "bWS", 128 * h, stop=False)
+
     for t in range(R):
-        src, win = ("bX", XW) if t else ("bU", M)
         if t:
-            banks = [4, 5, 6, 7, 2, 3, 0, 1]
-            for k in range(8):
-                gather("V" if k in (0, 2) else "S", "bG", UW * k, UW, "bX", XW, "bCT16", 16 * k)
-                if k == 5 and t == 1:
-                    for h in range(2):
-                        copy("S", "bTT", 256 * h, "P%d" % h, 0, 256)
-            if t == 2:
-                for h in range(2):
-                    tt("bTT", 256 * h, "P%d" % h, 0, "bTT", 256 * h, 256, A.add)
-            for k in range(8):
-                p = "P%d" % banks[k]
-                mm(p, 0, UW, "bKEF", 0, 128, "bG", UW * k)
-                tt("bV", UW * k, p, 0, "bS", UW * k, UW, A.mult)
-        gather("S", "bWS", 0, 256, "bV", E + 16, "bLS16", 0)
-        gather("V", "bWS", 256, 256, "bV", E + 16, "bLS16", 16)
-        for s in range(8):
+            units = [(0, 128, "V"), (128, 128, "S"), (256, 256, "S"), (512, 256, "V"), (768, 256, "S"), (1024, 256, "S"),
+                     (1280, 256, "S"), (1536, 256, "S"), (1792, 256, "S")]
+            for a, n, q in units:
+                gather(q, "bG", a, n, "bX", XW, "bCT16", a // 16)
+            outs = [(256 * k, 256) for k in range(7)] + [(1792, 128), (1920, 128)]
+            for (a, n), b in zip(outs, [4, 5, 6, 7, 0, 1, 2, 3, 4]):
+                mm("P%d" % b, 0, n, "bKEF", 0, 128, "bG", a)
+                tt("bV", a, "P%d" % b, 0, "bS", a, n, A.mult)
+        for h in range(2):
+            gather("S", "bWS", 128 * h, 128, "bV", E + 16, "bLS16", 8 * h)
+            gather("V", "bWS", 256 + 128 * h, 128, "bV", E + 16, "bLS16", 16 + 8 * h)
+        for s in (0, 1, 4, 5, 2, 3, 6, 7):
             mm("P6", 0, 64, "bLM", 112 - 16 * s, 128, "bWS", 64 * s, start=s == 0, stop=s == 7)
         if t == 0:
             copy("V", "bI16", 0, "bIT", 0, MC)
-            for k in range(R):
-                fill("bR%d" % k, 8 * rank, 8, 0.0)
-            fill("bEW", 512, 16, 0.0)
-            ts("bMN", 0, "bICOL", 0, 32, T.bAF[:, 5:6], None, A.is_equal, r=[("bAF", 5, 6)])
-            tt("bRN", 0, "bSHW", 0, "bMN", 0, 32, A.mult)
-            ts("bK", 2, "bAF", 5, 1, 8.0, None, A.mult)
-            ts("bVAL", 0, "bBS", 0, 64, T.bK[:, 2:3], None, A.add, r=[("bK", 2, 3)])
-            oo = T.bISH[:, 0:ME].indirect(T.bCP16[:, 128:132])
-            op("V", lambda e: e.tensor_copy(out=oo, in_=T.bVAL[:, :]), [("bVAL", 0, 64), ("bCP16", 128, 132)], [("bISH", 0, ME)])
         gather("S", "bW2", 0, BW, "bV", E + 16, "bI16", 0)
         copy("S", "bSD%d" % t, 0, "P6", 0, 64)
         send(t)
-        order = [0, 4, 5, 1, 2, 3]
-        for k in order[1:]:
-            gather("V" if k > 3 else "S", "bW2", BW * k, BW, "bV", E + 16, "bI16", 28 * k)
-        for k in order:
-            mm("P%d" % k, 0, BW, "bB", 0, 128, "bW2", BW * k)
         if t == 0:
-            mm("P7", 0, 32, "bB", 0, 128, "bRN", 0)
-            copy("V", "bNLN", 0, "P7", 0, 32)
-            gather("S", "bDR", 0, 512, "bISH", ME, "bNLX", 0)
-            dma([("Y", T.bDT[:, :], T.bDR[0:128:16, :])], "dd", [("bDR", 0, 512)], [("bDT", 0, 32)])
-            gather("S", "bNR", 0, 512, "bPOS", ME, "bNLX", 0)
-            dma([("Y", T.bNT[:, :], T.bNR[0:128:16, :])], "dn", [("bNR", 0, 512)], [("bNT", 0, 32)])
             for q in others:
                 oq = T.bPOS[:, 0:ME].indirect(T.bNLN[:, 4 * q:4 * q + 4])
                 op("V", lambda e: e.tensor_scalar(out=oq, in0=T.bBS[:, :], scalar1=1.0, scalar2=float(XS + 8 * q), op0=A.mult, op1=A.add),
                    [("bBS", 0, 64), ("bNLN", 4 * q, 4 * q + 4)], [("bPOS", 0, ME)])
-            for s in range(8):
-                oe, se = T.bEX[:, 128 * s:128 * s + 128], T.bMN[:, 4 * s:4 * s + 1]
-                op("S", lambda e: e.activation(out=oe, in_=T.bB[:, :], func=AF.Copy, scale=se), [("bB", 0, 128), ("bMN", 4 * s, 4 * s + 1)], [("bEX", 128 * s, 128 * s + 128)])
+            gather("S", "bW2", BW, BW, "bV", E + 16, "bI16", 28)
             gather("S", "bE1", 0, 1024, "bPOS", ME, "bCP16", 0)
             gather("V", "bE1", 1024, 1024, "bPOS", ME, "bCP16", 64)
             for i in range(16):
@@ -324,33 +308,50 @@ def rank_program(g, core, T, topo):
                         f = lambda e: e.tensor_copy(out=o2, in_=i2)
                     op(q, f, [("bE1", 1024 * h, 1024 * h + 1024)], [("bE2", 128 * i + 64 * h, 128 * i + 64 * h + 64)])
             dma([("Y", T.bCT[:, :], T.bE2[0:128:16, :])], "dct", [("bE2", 0, E)], [("bCT", 0, 128)])
+            ts("bK", 2, "bAF", 4, 1, 8.0, None, A.mult)
+            ts("bVAL", 0, "bBS", 0, 64, T.bK[:, 2:3], None, A.add, r=[("bK", 2, 3)])
+            oo = T.bISH[:, 0:ME].indirect(T.bCP16[:, 128:132])
+            op("V", lambda e: e.tensor_copy(out=oo, in_=T.bVAL[:, :]), [("bVAL", 0, 64), ("bCP16", 128, 132)], [("bISH", 0, ME)])
+            gather("S", "bDR", 0, 512, "bISH", ME, "bNLX", 0)
+            dma([("Y", T.bDT[:, :], T.bDR[0:128:16, :])], "dd", [("bDR", 0, 512)], [("bDT", 0, 32)])
+            order = [0, 1, 4, 2, 5, 3]
+            for k in order[2:]:
+                gather("V" if k > 3 else "S", "bW2", BW * k, BW, "bV", E + 16, "bI16", 28 * k)
+            ts("bN16", 0, "bNT", 0, 32, float(M - 1), None, A.min)
+            gather("S", "bX", XS, 512, "bU", M, "bN16", 0)
+        else:
+            order = [0, 4, 5, 1, 2, 3]
+            for k in order[1:]:
+                gather("V" if k > 3 else "S", "bW2", BW * k, BW, "bV", E + 16, "bI16", 28 * k)
+        for z, (b, k) in enumerate(zip([4, 5, 7, 6, 4, 5], order)):
+            if t == 0 and z == 2:
+                own_slots()
+            mm("P%d" % b, 0, BW, "bB", 0, 128, "bW2", BW * k)
+            tt("bX", BW * k, "P%d" % b, 0, "bX" if t else "bU", BW * k, BW, A.add)
+        if t:
+            own_slots()
+        if t == 0:
+            copy("V", "bD16", 0, "bDT", 0, 32)
             dma([("Y", T.bPT[:, :], T.bPOS[0:128:16, :])], "dpt", [("bPOS", 0, ME)], [("bPT", 0, MC)])
             dma([("Y", T.bPL[16 * k:16 * k + 16, 0:21], T.bPT[16 * k:16 * k + 16, 21 * k:21 * k + 21]) for k in range(8)],
                 "dpl", [("bPT", 0, MC)], [("bPL", 0, 21)])
-        for k in order:
-            tt("bX", BW * k, "P%d" % k, 0, "bX" if t else "bU", BW * k, BW, A.add)
-        if t == 0:
-            ts("bN16", 0, "bNT", 0, 32, float(M - 1), None, A.min)
-            copy("V", "bD16", 0, "bDT", 0, 32)
-            gather("S", "bTM", 0, 256, "bX", M, "bN16", 0)
-            gather("V", "bTM", 256, 256, "bX", M, "bN16", 16)
-        else:
-            ix = T.bX[:, 0:M].indirect(T.bN16[:, 0:32])
-            op("V", lambda e: e.tensor_tensor(out=T.bTM[:, :], in0=ix, in1=T.bTT[:, :], op=A.add),
-               [("bX", 0, M), ("bN16", 0, 32), ("bTT", 0, 512)], [("bTM", 0, 512)])
+        if t == 1:
+            copy("V", "bPL16", 0, "bPL", 0, 21)
         for s in range(8):
-            mm("P%d" % (7 - s // 4), 64 * (s % 4), 64, "bEX", 128 * s, 128, "bR%d" % t, 0)
+            p, c = (("P7", 64 * s), ("P6", 64 * (s - 4)), ("P5", 64 * (s - 6)))[(s > 3) + (s > 5)]
+            mm(p, c, 64, "bEX", 128 * s, 128, "bR%d" % t, 0)
         copy("S", "bEW", 0, "P7", 0, 256)
-        copy("V", "bEW", 256, "P6", 0, 256)
-        gather("S", "bWT", 0, 256, "bEW", 528, "bD16", 0)
-        gather("V", "bWT", 256, 256, "bEW", 528, "bD16", 16)
+        copy("V", "bEW", 256, "P6", 0, 128)
+        copy("V", "bEW", 384, "P5", 0, 128)
         for h in range(2):
-            mm("P%d" % h, 0, 256, "bB", 0, 128, "bWT", 256 * h)
-        for h in range(2):
-            tt("bX", XS + 256 * h, "P%d" % h, 0, "bTM", 256 * h, 256, A.add)
+            gather("S", "bWT", 128 * h, 128, "bEW", 528, "bD16", 8 * h)
+            gather("V", "bWT", 256 + 128 * h, 128, "bEW", 528, "bD16", 16 + 8 * h)
         if t == 0:
             copy("V", "bCT16", 0, "bCT", 0, 128)
-            copy("V", "bPL16", 0, "bPL", 0, 21)
+        for h in (0, 2, 1, 3):
+            mm("P%d" % h, 0, 128, "bB", 0, 128, "bWT", 128 * h, start=False)
+        for h in (0, 2, 1, 3):
+            tt("bX", XS + 128 * h, "P%d" % h, 0, "bX", XS + 128 * h, 128, A.add)
     gather("S", "bYG", 0, 160, "bX", XW, "bPL16", 0)
     gather("V", "bYG", 160, 176, "bX", XW, "bPL16", 10)
     dma([("YS"[k % 2], T.y[:, 336 * k:336 * k + 336], T.bYG[16 * k:16 * k + 16, :]) for k in range(8)], "dy", [("bYG", 0, 336)], [])

@@ -7,7 +7,9 @@ ME = 16 * MC
 XS = M
 XW = M + N * CAPP
 BW = 448
-NF = 1752
+BLOCKS = [(BW * k, BW) for k in range(5)] + [(2240, 256), (2496, 192)]
+NV, NS = 1500, 384
+Z = 688
 F32, BF, I32, U16 = "float32", "bfloat16", "int32", "uint16"
 
 
@@ -20,20 +22,21 @@ SCRATCH = {
     "bC16": sb(128, U16), "bCP16": sb(132, U16),
     "bIP": sb(1, I32), "bAI": sb(8, I32), "bAF": sb(8), "bK": sb(4), "bIMOD": sb(128), "bICOL": sb(32),
     "bJ": sb(128, BF), "bSB": sb(128, BF), "bYB": sb(128, BF), "bB": sb(128), "bB2": sb(128), "bMN": sb(32), "bMX": sb(32),
-    "bSHW": sb(32), "bRX": sb(32), "bRN": sb(32), "bNLX": sb(32, U16), "bNLN": sb(32, U16), "bLM": sb(240), "bEX": sb(1024),
+    "bSHW": sb(32), "bRX": sb(32), "bRN": sb(32), "bNLX": sb(32, U16), "bNLN": sb(32, U16), "bLM": sb(136),
     "bKEI": sb(8, BF), "bKEF": sb(128), "bKEB": sb(128, BF), "bON": sb(128, BF), "bWR": sb(M, BF), "bSTR": sb(E, BF),
     "bU": sb(M, BF), "bW": sb(M, BF), "bWG": sb(E), "bS": sb(E),
     "bG0": sb(E, BF), "bG": sb(E), "bV": sb(E + 16), "bWS": sb(512), "bW2": sb(M), "bX": sb(XW),
-    "bSD0": sb(64), "bSD1": sb(64), "bSD2": sb(64), "bR0": sb(64), "bR1": sb(64), "bR2": sb(64),
-    "bEW": sb(528), "bWT": sb(512), "bYG": sb(336),
-    "bEI": sb(E), "bINV": sb(ME), "bISH": sb(ME), "bPOS": sb(ME), "bBS": sb(64), "bVAL": sb(64),
+    "bSD0": sb(64), "bSD1": sb(64), "bSD2": sb(64), "bEW0": sb(80), "bEW1": sb(80), "bEW2": sb(80),
+    "bQ0": ("dram", [N, 128, 8], F32), "bQ1": ("dram", [N, 128, 8], F32), "bQ2": ("dram", [N, 128, 8], F32),
+    "bWT": sb(512), "bYG": sb(336),
+    "bEI": sb(E), "bINV": sb(ME), "bISH": sb(ME), "bPOS": sb(ME), "bBS": sb(64), "bBE": sb(64),
     "bLSR": sb(512), "bDR": sb(512), "bNR": sb(512), "bLST": sb(32), "bDT": sb(32), "bNT": sb(32),
     "bLS16": sb(32, U16), "bD16": sb(32, U16), "bN16": sb(32, U16), "bIT": sb(MC), "bI16": sb(MC, U16),
     "bPT": sb(MC), "bPL": sb(22), "bPL16": sb(22, U16), "bE1": sb(E), "bE2": sb(E), "bCT": sb(128), "bCT16": sb(128, U16),
 }
 SCRATCH.update({"P%d" % k: ("psum", [128, 512], F32) for k in range(8)})
 SEMAPHORES = ["kV", "kS", "kP", "kG", "loc", "arr0", "arr1", "arr2", "dconn", "dshare", "dke", "dw", "dst", "du",
-              "dinv", "dls", "dd", "dn", "dct", "dpt", "dpl", "dy"]
+              "dish", "dew0", "dew1", "dew2", "dinv", "dls", "dd", "dn", "dct", "dpt", "dpl", "dy"]
 A = AluOpType
 AF = ActivationFunctionType
 
@@ -159,24 +162,41 @@ def rank_program(g, core, T, topo):
     dma([("Y", T.bSTR[0:1, :], T.st[:, :])], "dst", [], [("bSTR", 0, E)])
     dma([("YS"[k % 2], T.bU[16 * k:16 * k + 16, :], T.u[:, :]) for k in range(8)], "du", [], [("bU", 0, M)])
     fill("bON", 0, 128, 1.0)
+    fill("bINV", 0, NV, float(E))
     iota("bIP", 0, 1, [[0, 1]], 0, 1, flag=False)
     iota("bEI", 0, 256, [[1, 256]], 0, 0)
-    iota("bICOL", 0, 32, [[1, 8], [0, 4]], 0, 0)
-    iota("bIMOD", 0, 128, [[0, 8], [1, 16]], 0, 0)
-    iota("bINV", NF, ME - NF, [[0, ME - NF]], E, 0)
+    iota("bINV", NV + NS, ME - NV - NS, [[0, ME - NV - NS]], E, 0)
     select("bJ", 16, "bON", [[0, 8], [1, 16]])
     select("bSB", 8, "bON", [[1, 8], [0, 16]])
+    iota("bICOL", 0, 32, [[1, 8], [0, 4]], 0, 0)
+    iota("bIMOD", 0, 128, [[0, 8], [1, 16]], 0, 0)
     iota("bV", E, 16, [[0, 16]], 0, 0)
-    iota("bEW", 512, 16, [[0, 16]], 0, 0)
-    iota("bLM", 0, 240, [[0, 240]], 0, 0)
-    for k in range(R):
-        iota("bR%d" % k, 8 * rank, 8, [[0, 8]], 0, 0)
+    iota("bLM", 0, 136, [[0, 136]], 0, 0)
+    iota("bISH", 0, Z, [[0, Z]], 64, 0)
+    dma([("Y", T.bISH[:, Z * k:Z * k + Z], T.bISH[:, 0:Z]) for k in range(1, 4)], "dish", [("bISH", 0, Z)], [("bISH", Z, ME)])
     iota("bPOS", 0, ME, [[1, 16], [16, MC]], 0, 0)
-    iota("bBS", 0, 32, [[256, 2], [64, 4], [2, 4]], 0, 0)
-    iota("bBS", 32, 32, [[256, 2], [64, 4], [2, 4]], 1, 0)
-    iota("bISH", 0, ME, [[0, ME]], 512, 0)
-
-    fill("bINV", 0, NF, float(E))
+    for h in range(2):
+        iota("bBS", 32 * h, 32, [[256, 2], [64, 4], [2, 4]], h, 0)
+        iota("bBE", 32 * h, 32, [[32, 2], [8, 4], [2, 4]], h, 0)
+    for k in range(R):
+        iota("bEW%d" % k, 0, 80, [[0, 80]], 0, 0)
+    for k in range(NS // 128):
+        o = T.bINV[:, NV + 128 * k:NV + 128 * k + 128]
+        op("S", lambda e: e.activation(out=o, in_=T.bON[:, 0:128], func=AF.Copy, scale=0.0, bias=float(E)),
+           [("bON", 0, 128)], [("bINV", NV + 128 * k, NV + 128 * k + 128)])
+    for n in (256, 512, 1024):
+        o, i, b = T.bEI[:, n:2 * n], T.bEI[:, 0:n], float(n)
+        op("S", lambda e: e.activation(out=o, in_=i, func=AF.Copy, bias=b), [("bEI", 0, n)], [("bEI", n, 2 * n)])
+    ts("bC1", 0, "bCI", 0, 132, 15, None, A.bitwise_and)
+    ts("bC2", 0, "bCI", 0, 132, 4, None, A.logical_shift_right)
+    ts("bC3", 0, "bC1", 0, 132, float(MC), None, A.mult)
+    copy("V", "bC16", 0, "bCI", 0, 128)
+    tt("bCPF", 0, "bC3", 0, "bC2", 0, 132, A.add)
+    copy("V", "bCP16", 0, "bCPF", 0, 132)
+    for h in range(2):
+        oi, ei = T.bINV[:, 0:ME].indirect(T.bCP16[:, 64 * h:64 * h + 64]), T.bEI[:, 1024 * h:1024 * h + 1024]
+        op("V", lambda e: e.tensor_copy(out=oi, in_=ei), [("bEI", 1024 * h, 1024 * h + 1024), ("bCP16", 64 * h, 64 * h + 64)], [("bINV", 0, ME)])
+    dma([("Y", T.bIT[:, :], T.bINV[0:128:16, :])], "dinv", [("bINV", 0, ME)], [("bIT", 0, MC)])
     for c, (o0, a0, o1, a1) in enumerate([(A.logical_shift_right, 4, A.bitwise_and, 1), (A.bitwise_and, 3, None, 0),
                                           (A.logical_shift_right, 2, A.bitwise_and, 3), (A.logical_shift_right, 5, None, 0),
                                           (A.logical_shift_right, 4, None, 0)]):
@@ -185,20 +205,8 @@ def rank_program(g, core, T, topo):
     ts("bK", 0, "bAF", 0, 1, 4.0, T.bAF[:, 1:2], A.mult, A.add, r=[("bAF", 1, 2)])
     ts("bK", 1, "bAF", 2, 1, 4.0, T.bAF[:, 3:4], A.mult, A.add, r=[("bAF", 3, 4)])
     ts("bMX", 0, "bICOL", 0, 32, T.bK[:, 0:1], None, A.is_equal, r=[("bK", 0, 1)])
-    ts("bMN", 0, "bICOL", 0, 32, T.bAF[:, 4:5], None, A.is_equal, r=[("bAF", 4, 5)])
     ts("bB2", 0, "bIMOD", 0, 128, T.bK[:, 1:2], None, A.is_equal, r=[("bK", 1, 2)])
-    for n in (256, 512, 1024):
-        o, i, b = T.bEI[:, n:2 * n], T.bEI[:, 0:n], float(n)
-        op("S", lambda e: e.activation(out=o, in_=i, func=AF.Copy, bias=b), [("bEI", 0, n)], [("bEI", n, 2 * n)])
-    ts("bC1", 0, "bCI", 0, 132, 15, None, A.bitwise_and)
-    ts("bC2", 0, "bCI", 0, 132, 4, None, A.logical_shift_right)
-    ts("bC3", 0, "bC1", 0, 132, float(MC), None, A.mult)
-    tt("bCPF", 0, "bC3", 0, "bC2", 0, 132, A.add)
-    copy("V", "bCP16", 0, "bCPF", 0, 132)
-    copy("V", "bC16", 0, "bCI", 0, 128)
-    oi = T.bINV[:, 0:ME].indirect(T.bCP16[:, 0:128])
-    op("V", lambda e: e.tensor_copy(out=oi, in_=T.bEI[:, :]), [("bEI", 0, E), ("bCP16", 0, 128)], [("bINV", 0, ME)])
-    dma([("Y", T.bIT[:, :], T.bINV[0:128:16, :])], "dinv", [("bINV", 0, ME)], [("bIT", 0, MC)])
+    ts("bMN", 0, "bICOL", 0, 32, T.bAF[:, 4:5], None, A.is_equal, r=[("bAF", 4, 5)])
     for k in range(6):
         mm("P%d" % k, 0, BW, "bON", 0, 128, "bWR", BW * k, rows=1)
         copy("S", "bW", BW * k, "P%d" % k, 0, BW, scale=-1.0)
@@ -234,13 +242,9 @@ def rank_program(g, core, T, topo):
     for k in range(4):
         tt("bV", 512 * k, "P%d" % (4 + k), 0, "bS", 512 * k, 512, A.mult)
     copy("V", "bLS16", 0, "bLST", 0, 32)
-    copy("S", "bLM", 112, "bB", 0, 16)
+    op("S", lambda e: e.activation(out=T.bLM[:, 7:128:8], in_=T.bB[:, 0:16], func=AF.Copy), [("bB", 0, 16)], [("bLM", 0, 136)])
     gather("S", "bNR", 0, 512, "bPOS", ME, "bNLX", 0)
     dma([("Y", T.bNT[:, :], T.bNR[0:128:16, :])], "dn", [("bNR", 0, 512)], [("bNT", 0, 32)])
-    for s in range(8):
-        oe, se = T.bEX[:, 128 * s:128 * s + 128], T.bMN[:, 4 * s:4 * s + 1]
-        op("S", lambda e: e.activation(out=oe, in_=T.bB[:, :], func=AF.Copy, scale=se),
-           [("bB", 0, 128), ("bMN", 4 * s, 4 * s + 1)], [("bEX", 128 * s, 128 * s + 128)])
     copy("S", "bKEF", 0, "bKEB", 0, 128)
 
     others = [q for q in range(N) if q != rank]
@@ -259,17 +263,53 @@ def rank_program(g, core, T, topo):
             rid, pid, _ = topo.addr(T.cores[q])
             tr.append(RemoteDMATransfer(dst_ids=[DstId(rid=rid, pnc=pid)], dma_engine_mask=sum(1 << e for e in lanes[q]),
                                         remote_sem=T.sem["arr%d" % t], src=T["bSD%d" % t][:, 8 * q:8 * q + 8],
-                                        dst=T["bR%d" % t][:, 8 * rank:8 * rank + 8]))
+                                        dst=T["bQ%d" % t][rank]))
         g.remote_dma_fused(tr, local_sem=T.sem["loc"])
         count["loc"] = count.get("loc", 0) + per * len(tr)
         s = "arr%d" % t
         count[s] = per * len(tr)
         for q in others:
-            wr["bR%d" % t] = wr.get("bR%d" % t, []) + [(8 * q, 8 * q + 8, s, count[s])]
+            wr["bQ%d" % t] = wr.get("bQ%d" % t, []) + [(q, q + 1, s, count[s])]
 
-    def own_slots():
+    def landed(t):
+        dma([("Y", T["bEW%d" % t][16 * a:16 * b, 0:64], T["bQ%d" % t][a:b]) for a, b in ((0, rank), (rank + 1, N)) if a < b],
+            "dew%d" % t, [("bQ%d" % t, 0, N)], [("bEW%d" % t, 0, 64)])
+
+    def ngather(q, k):
+        a, n = BLOCKS[k]
+        gather(q, "bW2", a, n, "bV", E + 16, "bI16", a // 16)
+
+    def node(k):
+        a, n = BLOCKS[k]
+        mm("P%d" % [4, 5, 7, 6][k % 4], 0, n, "bB", 0, 128, "bW2", a)
+
+    def nadd(t, k):
+        a, n = BLOCKS[k]
+        tt("bX", a, "P%d" % [4, 5, 7, 6][k % 4], 0, "bX" if t else "bU", a, n, A.add)
+
+    def shared(t):
         for h in range(4):
-            mm("P%d" % h, 0, 128, "bB", 0, 128, "bWS", 128 * h, stop=False)
+            x, y, z = T["bEW%d" % t][:, 0:80].indirect(T.bD16[:, 8 * h:8 * h + 8]), T.bWS[:, 128 * h:128 * h + 128], T.bWT[:, 128 * h:128 * h + 128]
+            op("V", lambda e: e.tensor_tensor(out=z, in0=x, in1=y, op=A.add),
+               [("bEW%d" % t, 0, 80), ("bD16", 8 * h, 8 * h + 8), ("bWS", 128 * h, 128 * h + 128)], [("bWT", 128 * h, 128 * h + 128)])
+
+    def ssum():
+        for h in range(4):
+            mm("P%d" % h, 0, 128, "bB", 0, 128, "bWT", 128 * h)
+
+    def sadd():
+        for h in range(4):
+            tt("bX", XS + 128 * h, "P%d" % h, 0, "bX", XS + 128 * h, 128, A.add)
+
+    def permute(q, i):
+        o, x = T.bE2[:, 128 * i:128 * i + 128], T.bE1[:, i:E:16]
+        if q == "S":
+            f = lambda e: e.activation(out=o, in_=x, func=AF.Copy)
+        elif q == "V":
+            f = lambda e: e.tensor_copy(out=o, in_=x)
+        else:
+            f = lambda e: e.affine_select(o, x, [[0, 128]], A.is_gt, 0.0, 1, 0)
+        op(q, f, [("bE1", 0, E)], [("bE2", 128 * i, 128 * i + 128)])
 
     for t in range(R):
         if t:
@@ -285,73 +325,73 @@ def rank_program(g, core, T, topo):
             gather("S", "bWS", 128 * h, 128, "bV", E + 16, "bLS16", 8 * h)
             gather("V", "bWS", 256 + 128 * h, 128, "bV", E + 16, "bLS16", 16 + 8 * h)
         for s in (0, 1, 4, 5, 2, 3, 6, 7):
-            mm("P6", 0, 64, "bLM", 112 - 16 * s, 128, "bWS", 64 * s, start=s == 0, stop=s == 7)
+            mm("P6", 0, 64, "bLM", 7 - s, 128, "bWS", 64 * s, start=s == 0, stop=s == 7)
         if t == 0:
             copy("V", "bI16", 0, "bIT", 0, MC)
-        gather("S", "bW2", 0, BW, "bV", E + 16, "bI16", 0)
+        ngather("S", 0)
         copy("S", "bSD%d" % t, 0, "P6", 0, 64)
         send(t)
         if t == 0:
+            oo = T.bISH[:, 0:ME].indirect(T.bCP16[:, 128:132])
+            op("V", lambda e: e.tensor_copy(out=oo, in_=T.bBE[:, :]), [("bBE", 0, 64), ("bCP16", 128, 132)], [("bISH", 0, ME)])
+            ngather("S", 1)
+            node(0)
+            node(1)
             for q in others:
                 oq = T.bPOS[:, 0:ME].indirect(T.bNLN[:, 4 * q:4 * q + 4])
                 op("V", lambda e: e.tensor_scalar(out=oq, in0=T.bBS[:, :], scalar1=1.0, scalar2=float(XS + 8 * q), op0=A.mult, op1=A.add),
                    [("bBS", 0, 64), ("bNLN", 4 * q, 4 * q + 4)], [("bPOS", 0, ME)])
-            gather("S", "bW2", BW, BW, "bV", E + 16, "bI16", 28)
+            ngather("S", 2)
+            node(2)
             gather("S", "bE1", 0, 1024, "bPOS", ME, "bCP16", 0)
             gather("V", "bE1", 1024, 1024, "bPOS", ME, "bCP16", 64)
             for i in range(16):
-                for q, h in (("S", 0), ("V", 1)):
-                    o2, i2 = T.bE2[:, 128 * i + 64 * h:128 * i + 64 * h + 64], T.bE1[:, 1024 * h + i:1024 * h + 1024:16]
-                    if q == "S":
-                        f = lambda e: e.activation(out=o2, in_=i2, func=AF.Copy)
-                    else:
-                        f = lambda e: e.tensor_copy(out=o2, in_=i2)
-                    op(q, f, [("bE1", 1024 * h, 1024 * h + 1024)], [("bE2", 128 * i + 64 * h, 128 * i + 64 * h + 64)])
-            dma([("Y", T.bCT[:, :], T.bE2[0:128:16, :])], "dct", [("bE2", 0, E)], [("bCT", 0, 128)])
-            ts("bK", 2, "bAF", 4, 1, 8.0, None, A.mult)
-            ts("bVAL", 0, "bBS", 0, 64, T.bK[:, 2:3], None, A.add, r=[("bK", 2, 3)])
-            oo = T.bISH[:, 0:ME].indirect(T.bCP16[:, 128:132])
-            op("V", lambda e: e.tensor_copy(out=oo, in_=T.bVAL[:, :]), [("bVAL", 0, 64), ("bCP16", 128, 132)], [("bISH", 0, ME)])
+                permute("GSVGVSGVGSVGVSGV"[i], i)
+            landed(t)
+            nadd(t, 0)
+            nadd(t, 1)
             gather("S", "bDR", 0, 512, "bISH", ME, "bNLX", 0)
             dma([("Y", T.bDT[:, :], T.bDR[0:128:16, :])], "dd", [("bDR", 0, 512)], [("bDT", 0, 32)])
-            order = [0, 1, 4, 2, 5, 3]
-            for k in order[2:]:
-                gather("V" if k > 3 else "S", "bW2", BW * k, BW, "bV", E + 16, "bI16", 28 * k)
+            dma([("Y", T.bCT[:, :], T.bE2[0:128:16, :])], "dct", [("bE2", 0, E)], [("bCT", 0, 128)])
+            ngather("S", 3)
+            node(3)
+            nadd(t, 2)
+            copy("V", "bD16", 0, "bDT", 0, 32)
+            for k in (4, 5, 6):
+                ngather("S", k)
             ts("bN16", 0, "bNT", 0, 32, float(M - 1), None, A.min)
             gather("S", "bX", XS, 512, "bU", M, "bN16", 0)
-        else:
-            order = [0, 4, 5, 1, 2, 3]
-            for k in order[1:]:
-                gather("V" if k > 3 else "S", "bW2", BW * k, BW, "bV", E + 16, "bI16", 28 * k)
-        for z, (b, k) in enumerate(zip([4, 5, 7, 6, 4, 5], order)):
-            if t == 0 and z == 2:
-                own_slots()
-            mm("P%d" % b, 0, BW, "bB", 0, 128, "bW2", BW * k)
-            tt("bX", BW * k, "P%d" % b, 0, "bX" if t else "bU", BW * k, BW, A.add)
-        if t:
-            own_slots()
-        if t == 0:
-            copy("V", "bD16", 0, "bDT", 0, 32)
+            nadd(t, 3)
+            node(4)
+            shared(t)
+            nadd(t, 4)
+            node(5)
+            ssum()
+            nadd(t, 5)
+            node(6)
+            sadd()
+            copy("V", "bCT16", 0, "bCT", 0, 128)
+            nadd(t, 6)
             dma([("Y", T.bPT[:, :], T.bPOS[0:128:16, :])], "dpt", [("bPOS", 0, ME)], [("bPT", 0, MC)])
             dma([("Y", T.bPL[16 * k:16 * k + 16, 0:21], T.bPT[16 * k:16 * k + 16, 21 * k:21 * k + 21]) for k in range(8)],
                 "dpl", [("bPT", 0, MC)], [("bPL", 0, 21)])
+        else:
+            landed(t)
+            ngather("V", 1)
+            for k in range(2, 7):
+                ngather("S", k)
+            for k in range(5):
+                node(k)
+                nadd(t, k)
+            shared(t)
+            node(5)
+            nadd(t, 5)
+            ssum()
+            node(6)
+            sadd()
+            nadd(t, 6)
         if t == 1:
             copy("V", "bPL16", 0, "bPL", 0, 21)
-        for s in range(8):
-            p, c = (("P7", 64 * s), ("P6", 64 * (s - 4)), ("P5", 64 * (s - 6)))[(s > 3) + (s > 5)]
-            mm(p, c, 64, "bEX", 128 * s, 128, "bR%d" % t, 0)
-        copy("S", "bEW", 0, "P7", 0, 256)
-        copy("V", "bEW", 256, "P6", 0, 128)
-        copy("V", "bEW", 384, "P5", 0, 128)
-        for h in range(2):
-            gather("S", "bWT", 128 * h, 128, "bEW", 528, "bD16", 8 * h)
-            gather("V", "bWT", 256 + 128 * h, 128, "bEW", 528, "bD16", 16 + 8 * h)
-        if t == 0:
-            copy("V", "bCT16", 0, "bCT", 0, 128)
-        for h in (0, 2, 1, 3):
-            mm("P%d" % h, 0, 128, "bB", 0, 128, "bWT", 128 * h, start=False)
-        for h in (0, 2, 1, 3):
-            tt("bX", XS + 128 * h, "P%d" % h, 0, "bX", XS + 128 * h, 128, A.add)
     gather("S", "bYG", 0, 160, "bX", XW, "bPL16", 0)
     gather("V", "bYG", 160, 176, "bX", XW, "bPL16", 10)
     dma([("YS"[k % 2], T.y[:, 336 * k:336 * k + 336], T.bYG[16 * k:16 * k + 16, :]) for k in range(8)], "dy", [("bYG", 0, 336)], [])

@@ -7,9 +7,9 @@ ME = 16 * MC
 XS = M
 XW = M + N * CAPP
 BW = 448
-BLOCKS = [(BW * k, BW) for k in range(5)] + [(2240, 256), (2496, 192)]
+BLOCKS = [(BW * k, BW) for k in range(5)] + [(2240, 288), (2528, 160)]
 NV, NS = 1500, 384
-Z = 688
+Z = 344
 F32, BF, I32, U16 = "float32", "bfloat16", "int32", "uint16"
 
 
@@ -20,10 +20,10 @@ def sb(n, d=F32):
 SCRATCH = {
     "bCI": sb(132, I32), "bC1": sb(132, I32), "bC2": sb(132, I32), "bC3": sb(132, I32), "bCPF": sb(132),
     "bC16": sb(128, U16), "bCP16": sb(132, U16),
-    "bIP": sb(1, I32), "bAI": sb(8, I32), "bAF": sb(8), "bK": sb(4), "bIMOD": sb(128), "bICOL": sb(32),
-    "bJ": sb(128, BF), "bSB": sb(128, BF), "bYB": sb(128, BF), "bB": sb(128), "bB2": sb(128), "bMN": sb(32), "bMX": sb(32),
+    "bK8": sb(128, BF), "bK16": sb(128, BF), "bT8": sb(32, BF),
+    "bJ": sb(128, BF), "bSB": sb(128, BF), "bYB": sb(128, BF), "bB": sb(128), "bB2": sb(128),
     "bSHW": sb(32), "bRX": sb(32), "bRN": sb(32), "bNLX": sb(32, U16), "bNLN": sb(32, U16), "bLM": sb(136),
-    "bKEI": sb(8, BF), "bKEF": sb(128), "bKEB": sb(128, BF), "bON": sb(128, BF), "bWR": sb(M, BF), "bSTR": sb(E, BF),
+    "bKEI": sb(8, BF), "bKEF": sb(128), "bKEB": sb(128, BF), "bON": sb(128, BF), "bMO": sb(128, BF), "bSTR": sb(E, BF),
     "bU": sb(M, BF), "bW": sb(M, BF), "bWG": sb(E), "bS": sb(E),
     "bG0": sb(E, BF), "bG": sb(E), "bV": sb(E + 16), "bWS": sb(512), "bW2": sb(M), "bX": sb(XW),
     "bSD0": sb(64), "bSD1": sb(64), "bSD2": sb(64), "bEW0": sb(80), "bEW1": sb(80), "bEW2": sb(80),
@@ -35,7 +35,7 @@ SCRATCH = {
     "bPT": sb(MC), "bPL": sb(22), "bPL16": sb(22, U16), "bE1": sb(E), "bE2": sb(E), "bCT": sb(128), "bCT16": sb(128, U16),
 }
 SCRATCH.update({"P%d" % k: ("psum", [128, 512], F32) for k in range(8)})
-SEMAPHORES = ["kV", "kS", "kP", "kG", "loc", "arr0", "arr1", "arr2", "dconn", "dshare", "dke", "dw", "dst", "du",
+SEMAPHORES = ["kV", "kS", "kP", "kG", "loc", "arr0", "arr1", "arr2", "dconn", "dshare", "dke", "dw", "dw2", "dst", "du",
               "dish", "dew0", "dew1", "dew2", "dinv", "dls", "dd", "dn", "dct", "dpt", "dpl", "dy"]
 A = AluOpType
 AF = ActivationFunctionType
@@ -117,20 +117,16 @@ def rank_program(g, core, T, topo):
         else:
             op("S", lambda e: e.activation(out=o, in_=i, func=AF.Copy), r, [(dst, a, a + n)])
 
-    def copy(q, dst, a, src, b, n, rows=128, scale=1.0):
+    def copy(q, dst, a, src, b, n, rows=128):
         o, i = T[dst][0:rows, a:a + n], T[src][0:rows, b:b + n]
         if q == "V":
             op("V", lambda e: e.tensor_copy(out=o, in_=i), [(src, b, b + n)], [(dst, a, a + n)])
         else:
-            op("S", lambda e: e.activation(out=o, in_=i, func=AF.Copy, scale=scale), [(src, b, b + n)], [(dst, a, a + n)])
+            op("S", lambda e: e.activation(out=o, in_=i, func=AF.Copy), [(src, b, b + n)], [(dst, a, a + n)])
 
-    def ts(dst, a, src, b, n, s1, s2, op0, op1=None, r=(), rows=128):
-        o, i = T[dst][0:rows, a:a + n], T[src][0:rows, b:b + n]
-        if op1 is None:
-            f = lambda e: e.tensor_scalar(out=o, in0=i, scalar1=s1, scalar2=None, op0=op0)
-        else:
-            f = lambda e: e.tensor_scalar(out=o, in0=i, scalar1=s1, scalar2=s2, op0=op0, op1=op1)
-        op("V", f, [(src, b, b + n)] + list(r), [(dst, a, a + n)])
+    def ts(dst, a, src, b, n, s1, op0):
+        o, i = T[dst][:, a:a + n], T[src][:, b:b + n]
+        op("V", lambda e: e.tensor_scalar(out=o, in0=i, scalar1=s1, scalar2=None, op0=op0), [(src, b, b + n)], [(dst, a, a + n)])
 
     def tt(dst, a, s0, b, s1, c, n, o):
         x, y, z = T[dst][:, a:a + n], T[s0][:, b:b + n], T[s1][:, c:c + n]
@@ -143,43 +139,41 @@ def rank_program(g, core, T, topo):
         o, l, x = T[dst][0:m, a:a + n], T[lh][0:rows, la:la + m], T[rh][0:rows, ra:ra + n]
         op("P", lambda e: e.matmul(o, l, x, start, stop), [(lh, la, la + m), (rh, ra, ra + n)], [(dst, a, a + n)])
 
-    def iota(dst, a, n, pat, base, cm, rows=128, flag=True):
-        o = T[dst][0:rows, a:a + n]
-        if flag:
-            f = lambda e: e.iota(o, pat, base, cm, allow_small_or_imprecise_dtypes=True)
-        else:
-            f = lambda e: e.iota(o, pat, base, cm)
-        op("G", f, [], [(dst, a, a + n)])
+    def iota(dst, a, n, pat, base, cm):
+        o = T[dst][:, a:a + n]
+        op("G", lambda e: e.iota(o, pat, base, cm, allow_small_or_imprecise_dtypes=True), [], [(dst, a, a + n)])
 
-    def select(dst, rows, src, pat):
-        o, i = T[dst][0:rows, 0:128], T[src][0:rows, 0:128]
-        op("G", lambda e: e.affine_select(o, i, pat, A.is_equal, 0.0, 0, -1), [(src, 0, 128)], [(dst, 0, 128)])
+    def select(dst, rows, a, n, pat, base=0):
+        o, i = T[dst][0:rows, a:a + n], T.bON[0:rows, 0:n]
+        op("G", lambda e: e.affine_select(o, i, pat, A.is_equal, 0.0, base, -1), [("bON", 0, n)], [(dst, a, a + n)])
 
     dma([("Y", T.bCI[:, 0:128], T.conn[:, :])], "dconn", [], [("bCI", 0, 128)])
     dma([("Y", T.bCI[:, 128:132], T.share[:, :])], "dshare", [], [("bCI", 128, 132)])
-    dma([("Y", T.bWR[0:1, :], T.w[:, :])], "dw", [], [("bWR", 0, M)])
+    dma([("Y", T.bW[k:k + 1, :], T.w[:, :]) for k in range(8)], "dw", [], [("bW", 0, M)])
     dma([("Y", T.bKEI[0:8, :], T.ke[:, :])], "dke", [], [("bKEI", 0, 8)])
     dma([("Y", T.bSTR[0:1, :], T.st[:, :])], "dst", [], [("bSTR", 0, E)])
     dma([("YS"[k % 2], T.bU[16 * k:16 * k + 16, :], T.u[:, :]) for k in range(8)], "du", [], [("bU", 0, M)])
+    dma([("Y", T.bW[8 * k:8 * k + 8, :], T.bW[0:8, :]) for k in range(1, 16)], "dw2", [("bW", 0, M)], [("bW", 0, M)])
     fill("bON", 0, 128, 1.0)
+    fill("bMO", 0, 128, -1.0)
     fill("bINV", 0, NV, float(E))
-    iota("bIP", 0, 1, [[0, 1]], 0, 1, flag=False)
     iota("bEI", 0, 256, [[1, 256]], 0, 0)
     iota("bINV", NV + NS, ME - NV - NS, [[0, ME - NV - NS]], E, 0)
-    select("bJ", 16, "bON", [[0, 8], [1, 16]])
-    select("bSB", 8, "bON", [[1, 8], [0, 16]])
-    iota("bICOL", 0, 32, [[1, 8], [0, 4]], 0, 0)
-    iota("bIMOD", 0, 128, [[0, 8], [1, 16]], 0, 0)
+    select("bJ", 16, 0, 128, [[0, 8], [1, 16]])
+    select("bSB", 8, 0, 128, [[1, 8], [0, 16]])
+    select("bT8", 8, 0, 32, [[1, 8], [0, 4]])
+    for k in range(4):
+        select("bK8", 8, 32 * k, 32, [[4, 2], [0, 4], [1, 4]])
+        select("bK16", 16, 32 * k, 32, [[0, 2], [4, 4], [0, 4]], k)
     iota("bV", E, 16, [[0, 16]], 0, 0)
     iota("bLM", 0, 136, [[0, 136]], 0, 0)
     iota("bISH", 0, Z, [[0, Z]], 64, 0)
-    dma([("Y", T.bISH[:, Z * k:Z * k + Z], T.bISH[:, 0:Z]) for k in range(1, 4)], "dish", [("bISH", 0, Z)], [("bISH", Z, ME)])
+    dma([("Y", T.bISH[:, Z * k:Z * k + Z], T.bISH[:, 0:Z]) for k in range(1, 8)], "dish", [("bISH", 0, Z)], [("bISH", Z, ME)])
     iota("bPOS", 0, ME, [[1, 16], [16, MC]], 0, 0)
     for h in range(2):
         iota("bBS", 32 * h, 32, [[256, 2], [64, 4], [2, 4]], h, 0)
         iota("bBE", 32 * h, 32, [[32, 2], [8, 4], [2, 4]], h, 0)
-    for k in range(R):
-        iota("bEW%d" % k, 0, 80, [[0, 80]], 0, 0)
+    iota("bEW0", 0, 80, [[0, 80]], 0, 0)
     for k in range(NS // 128):
         o = T.bINV[:, NV + 128 * k:NV + 128 * k + 128]
         op("S", lambda e: e.activation(out=o, in_=T.bON[:, 0:128], func=AF.Copy, scale=0.0, bias=float(E)),
@@ -187,9 +181,9 @@ def rank_program(g, core, T, topo):
     for n in (256, 512, 1024):
         o, i, b = T.bEI[:, n:2 * n], T.bEI[:, 0:n], float(n)
         op("S", lambda e: e.activation(out=o, in_=i, func=AF.Copy, bias=b), [("bEI", 0, n)], [("bEI", n, 2 * n)])
-    ts("bC1", 0, "bCI", 0, 132, 15, None, A.bitwise_and)
-    ts("bC2", 0, "bCI", 0, 132, 4, None, A.logical_shift_right)
-    ts("bC3", 0, "bC1", 0, 132, float(MC), None, A.mult)
+    ts("bC1", 0, "bCI", 0, 132, 15, A.bitwise_and)
+    ts("bC2", 0, "bCI", 0, 132, 4, A.logical_shift_right)
+    ts("bC3", 0, "bC1", 0, 132, float(MC), A.mult)
     copy("V", "bC16", 0, "bCI", 0, 128)
     tt("bCPF", 0, "bC3", 0, "bC2", 0, 132, A.add)
     copy("V", "bCP16", 0, "bCPF", 0, 132)
@@ -197,19 +191,10 @@ def rank_program(g, core, T, topo):
         oi, ei = T.bINV[:, 0:ME].indirect(T.bCP16[:, 64 * h:64 * h + 64]), T.bEI[:, 1024 * h:1024 * h + 1024]
         op("V", lambda e: e.tensor_copy(out=oi, in_=ei), [("bEI", 1024 * h, 1024 * h + 1024), ("bCP16", 64 * h, 64 * h + 64)], [("bINV", 0, ME)])
     dma([("Y", T.bIT[:, :], T.bINV[0:128:16, :])], "dinv", [("bINV", 0, ME)], [("bIT", 0, MC)])
-    for c, (o0, a0, o1, a1) in enumerate([(A.logical_shift_right, 4, A.bitwise_and, 1), (A.bitwise_and, 3, None, 0),
-                                          (A.logical_shift_right, 2, A.bitwise_and, 3), (A.logical_shift_right, 5, None, 0),
-                                          (A.logical_shift_right, 4, None, 0)]):
-        ts("bAI", c, "bIP", 0, 1, a0, a1, o0, o1)
-    copy("V", "bAF", 0, "bAI", 0, 5)
-    ts("bK", 0, "bAF", 0, 1, 4.0, T.bAF[:, 1:2], A.mult, A.add, r=[("bAF", 1, 2)])
-    ts("bK", 1, "bAF", 2, 1, 4.0, T.bAF[:, 3:4], A.mult, A.add, r=[("bAF", 3, 4)])
-    ts("bMX", 0, "bICOL", 0, 32, T.bK[:, 0:1], None, A.is_equal, r=[("bK", 0, 1)])
-    ts("bB2", 0, "bIMOD", 0, 128, T.bK[:, 1:2], None, A.is_equal, r=[("bK", 1, 2)])
-    ts("bMN", 0, "bICOL", 0, 32, T.bAF[:, 4:5], None, A.is_equal, r=[("bAF", 4, 5)])
-    for k in range(6):
-        mm("P%d" % k, 0, BW, "bON", 0, 128, "bWR", BW * k, rows=1)
-        copy("S", "bW", BW * k, "P%d" % k, 0, BW, scale=-1.0)
+    for k in range(4):
+        mm("P%d" % k, 0, 512, "bMO", 0, 128, "bSTR", 512 * k, rows=1)
+    for k in (0, 1):
+        gather("S", "bG0", 512 * k, 512, "bU", M, "bC16", 32 * k)
     mm("P7", 0, 128, "bJ", 0, 128, "bJ", 0, rows=16)
     copy("S", "bB", 0, "P7", 0, 128)
     mm("P6", 0, 128, "bKEI", 0, 8, "bSB", 0, rows=8)
@@ -219,20 +204,22 @@ def rank_program(g, core, T, topo):
         copy("S", "bSHW", a, "bCPF", b, n)
     copy("S", "bSHW", 8, "bSHW", 0, 8)
     copy("S", "bSHW", 16, "bSHW", 0, 16)
+    for k in (2, 3):
+        gather("S", "bG0", 512 * k, 512, "bU", M, "bC16", 32 * k)
+    mm("P4", 0, 128, "bK16", 0, 128, "bJ", 0, rows=16)
+    copy("S", "bB2", 0, "P4", 0, 128)
+    mm("P5", 0, 32, "bK8", 0, 128, "bT8", 0, rows=8)
+    mm("P5", 32, 32, "bSB", 0, 128, "bT8", 0, rows=8)
     for k in range(4):
-        mm("P%d" % k, 0, 512, "bON", 0, 128, "bSTR", 512 * k, rows=1)
         gather("S", "bWG", 512 * k, 512, "bW", M, "bC16", 32 * k)
-    tt("bRX", 0, "bSHW", 0, "bMX", 0, 32, A.mult)
+    tt("bRX", 0, "bSHW", 0, "P5", 0, 32, A.mult)
     mm("P6", 0, 32, "bB2", 0, 128, "bRX", 0)
     tt("bKEB", 0, "P7", 0, "bB", 0, 128, A.mult)
-    tt("bRN", 0, "bSHW", 0, "bMN", 0, 32, A.mult)
-    for k in range(3):
-        gather("S", "bG0", 512 * k, 512, "bU", M, "bC16", 32 * k)
+    tt("bRN", 0, "bSHW", 0, "P5", 32, 32, A.mult)
     copy("V", "bNLX", 0, "P6", 0, 32)
     mm("P6", 0, 32, "bB", 0, 128, "bRN", 0)
     gather("S", "bLSR", 0, 512, "bINV", ME, "bNLX", 0)
     dma([("Y", T.bLST[:, :], T.bLSR[0:128:16, :])], "dls", [("bLSR", 0, 512)], [("bLST", 0, 32)])
-    gather("S", "bG0", 1536, 512, "bU", M, "bC16", 96)
     for k in range(4):
         tt("bS", 512 * k, "bWG", 512 * k, "P%d" % k, 0, 512, A.mult)
         if k == 0:
@@ -257,6 +244,7 @@ def rank_program(g, core, T, topo):
     lanes.update({q: eon[per * k:per * k + per] for k, q in enumerate(on)})
 
     def send(t):
+        copy("S", "bSD%d" % t, 0, "P3", 0, 64)
         wait("G", need("G", [("bSD%d" % t, 0, 64)], []))
         tr = []
         for q in off + on:
@@ -270,14 +258,17 @@ def rank_program(g, core, T, topo):
         count[s] = per * len(tr)
         for q in others:
             wr["bQ%d" % t] = wr.get("bQ%d" % t, []) + [(q, q + 1, s, count[s])]
+        if t + 1 < R:
+            iota("bEW%d" % (t + 1), 0, 80, [[0, 80]], 0, 0)
 
     def landed(t):
         dma([("Y", T["bEW%d" % t][16 * a:16 * b, 0:64], T["bQ%d" % t][a:b]) for a, b in ((0, rank), (rank + 1, N)) if a < b],
             "dew%d" % t, [("bQ%d" % t, 0, N)], [("bEW%d" % t, 0, 64)])
 
-    def ngather(q, k):
-        a, n = BLOCKS[k]
-        gather(q, "bW2", a, n, "bV", E + 16, "bI16", a // 16)
+    def ngather(q, *ks):
+        for k in ks:
+            a, n = BLOCKS[k]
+            gather(q, "bW2", a, n, "bV", E + 16, "bI16", a // 16)
 
     def node(k):
         a, n = BLOCKS[k]
@@ -301,92 +292,99 @@ def rank_program(g, core, T, topo):
         for h in range(4):
             tt("bX", XS + 128 * h, "P%d" % h, 0, "bX", XS + 128 * h, 128, A.add)
 
-    def permute(q, i):
-        o, x = T.bE2[:, 128 * i:128 * i + 128], T.bE1[:, i:E:16]
-        if q == "S":
-            f = lambda e: e.activation(out=o, in_=x, func=AF.Copy)
-        elif q == "V":
-            f = lambda e: e.tensor_copy(out=o, in_=x)
-        else:
-            f = lambda e: e.affine_select(o, x, [[0, 128]], A.is_gt, 0.0, 1, 0)
-        op(q, f, [("bE1", 0, E)], [("bE2", 128 * i, 128 * i + 128)])
+    def permute(q, *js):
+        for j in js:
+            o, x = T.bE2[:, 128 * j:128 * j + 128], T.bE1[:, j:E:16]
+            if q == "S":
+                f = lambda e: e.activation(out=o, in_=x, func=AF.Copy)
+            elif q == "V":
+                f = lambda e: e.tensor_copy(out=o, in_=x)
+            else:
+                f = lambda e: e.affine_select(o, x, [[0, 128]], A.is_gt, 0.0, 1, 0)
+            op(q, f, [("bE1", 0, E)], [("bE2", 128 * j, 128 * j + 128)])
 
     for t in range(R):
         if t:
-            units = [(0, 128, "V"), (128, 128, "S"), (256, 256, "S"), (512, 256, "V"), (768, 256, "S"), (1024, 256, "S"),
-                     (1280, 256, "S"), (1536, 256, "S"), (1792, 256, "S")]
+            units = [(0, 64, "V"), (64, 64, "S"), (128, 128, "V"), (256, 256, "S"), (512, 256, "V"), (768, 256, "S"),
+                     (1024, 256, "S"), (1280, 256, "S"), (1536, 256, "S"), (1792, 256, "S")]
             for a, n, q in units:
                 gather(q, "bG", a, n, "bX", XW, "bCT16", a // 16)
-            outs = [(256 * k, 256) for k in range(7)] + [(1792, 128), (1920, 128)]
-            for (a, n), b in zip(outs, [4, 5, 6, 7, 0, 1, 2, 3, 4]):
+            outs = [(0, 64), (64, 64), (128, 128)] + [(256 * k, 256) for k in range(1, 7)] + [(1792, 128), (1920, 64), (1984, 64)]
+            for (a, n), b in zip(outs, [4, 5, 6, 7, 0, 1, 2, 3, 4, 5, 6, 7]):
                 mm("P%d" % b, 0, n, "bKEF", 0, 128, "bG", a)
                 tt("bV", a, "P%d" % b, 0, "bS", a, n, A.mult)
-        for h in range(2):
-            gather("S", "bWS", 128 * h, 128, "bV", E + 16, "bLS16", 8 * h)
-            gather("V", "bWS", 256 + 128 * h, 128, "bV", E + 16, "bLS16", 16 + 8 * h)
-        for s in (0, 1, 4, 5, 2, 3, 6, 7):
-            mm("P6", 0, 64, "bLM", 7 - s, 128, "bWS", 64 * s, start=s == 0, stop=s == 7)
+        for a, n in ((0, 64), (64, 64), (128, 128)):
+            gather("S", "bWS", a, n, "bV", E + 16, "bLS16", a // 16)
+            gather("V", "bWS", 256 + a, n, "bV", E + 16, "bLS16", 16 + a // 16)
+        for s in (0, 4, 1, 5, 2, 6, 3, 7):
+            mm("P3", 0, 64, "bLM", 7 - s, 128, "bWS", 64 * s, start=s == 0, stop=s == 7)
         if t == 0:
+            send(t)
             copy("V", "bI16", 0, "bIT", 0, MC)
-        ngather("S", 0)
-        copy("S", "bSD%d" % t, 0, "P6", 0, 64)
-        send(t)
-        if t == 0:
-            oo = T.bISH[:, 0:ME].indirect(T.bCP16[:, 128:132])
-            op("V", lambda e: e.tensor_copy(out=oo, in_=T.bBE[:, :]), [("bBE", 0, 64), ("bCP16", 128, 132)], [("bISH", 0, ME)])
-            ngather("S", 1)
-            node(0)
-            node(1)
             for q in others:
                 oq = T.bPOS[:, 0:ME].indirect(T.bNLN[:, 4 * q:4 * q + 4])
                 op("V", lambda e: e.tensor_scalar(out=oq, in0=T.bBS[:, :], scalar1=1.0, scalar2=float(XS + 8 * q), op0=A.mult, op1=A.add),
                    [("bBS", 0, 64), ("bNLN", 4 * q, 4 * q + 4)], [("bPOS", 0, ME)])
-            ngather("S", 2)
+            ngather("S", 2, 1)
             node(2)
+            ngather("S", 0)
+            node(0)
+            oo = T.bISH[:, 0:ME].indirect(T.bCP16[:, 128:132])
+            op("V", lambda e: e.tensor_copy(out=oo, in_=T.bBE[:, :]), [("bBE", 0, 64), ("bCP16", 128, 132)], [("bISH", 0, ME)])
             gather("S", "bE1", 0, 1024, "bPOS", ME, "bCP16", 0)
             gather("V", "bE1", 1024, 1024, "bPOS", ME, "bCP16", 64)
-            for i in range(16):
-                permute("GSVGVSGVGSVGVSGV"[i], i)
-            landed(t)
-            nadd(t, 0)
-            nadd(t, 1)
+            node(1)
             gather("S", "bDR", 0, 512, "bISH", ME, "bNLX", 0)
             dma([("Y", T.bDT[:, :], T.bDR[0:128:16, :])], "dd", [("bDR", 0, 512)], [("bDT", 0, 32)])
-            dma([("Y", T.bCT[:, :], T.bE2[0:128:16, :])], "dct", [("bE2", 0, E)], [("bCT", 0, 128)])
-            ngather("S", 3)
+            permute("V", 5)
+            ngather("S", 3, 4)
             node(3)
-            nadd(t, 2)
-            copy("V", "bD16", 0, "bDT", 0, 32)
-            for k in (4, 5, 6):
-                ngather("S", k)
-            ts("bN16", 0, "bNT", 0, 32, float(M - 1), None, A.min)
-            gather("S", "bX", XS, 512, "bU", M, "bN16", 0)
-            nadd(t, 3)
+            landed(t)
+            permute("V", 1, 7, 3)
+            permute("G", 6, 15, 10, 14)
+            ngather("S", 5)
+            nadd(t, 0)
+            nadd(t, 1)
+            permute("V", 2)
+            permute("S", 4)
             node(4)
-            shared(t)
-            nadd(t, 4)
+            nadd(t, 2)
+            permute("V", 11)
             node(5)
+            copy("V", "bD16", 0, "bDT", 0, 32)
+            ts("bN16", 0, "bNT", 0, 32, float(M - 1), A.min)
+            permute("G", 12, 13, 9, 0)
+            shared(t)
+            permute("S", 8)
+            gather("S", "bX", XS, 512, "bU", M, "bN16", 0)
             ssum()
+            ngather("S", 6)
+            nadd(t, 4)
+            nadd(t, 3)
             nadd(t, 5)
             node(6)
             sadd()
+            dma([("Y", T.bCT[:, :], T.bE2[0:128:16, :])], "dct", [("bE2", 0, E)], [("bCT", 0, 128)])
             copy("V", "bCT16", 0, "bCT", 0, 128)
             nadd(t, 6)
             dma([("Y", T.bPT[:, :], T.bPOS[0:128:16, :])], "dpt", [("bPOS", 0, ME)], [("bPT", 0, MC)])
             dma([("Y", T.bPL[16 * k:16 * k + 16, 0:21], T.bPT[16 * k:16 * k + 16, 21 * k:21 * k + 21]) for k in range(8)],
                 "dpl", [("bPT", 0, MC)], [("bPL", 0, 21)])
         else:
+            ngather("S", 0)
+            send(t)
             landed(t)
             ngather("V", 1)
-            for k in range(2, 7):
-                ngather("S", k)
-            for k in range(5):
+            ngather("S", 2, 3, 4, 5, 6)
+            for k in range(4):
                 node(k)
                 nadd(t, k)
             shared(t)
+            node(4)
             node(5)
-            nadd(t, 5)
+            nadd(t, 4)
             ssum()
+            nadd(t, 5)
             node(6)
             sadd()
             nadd(t, 6)

from concourse.bass import DstId, RemoteDMATransfer
from concourse.mybir import AluOpType, ActivationFunctionType

E, M, CAPP, R, N = 2048, 2688, 64, 3, 8
MC = (M + CAPP) // 16
ME = 16 * MC
XS = M
XW = M + N * CAPP
BW = 448
BLOCKS = [(BW * k, BW) for k in range(5)] + [(2240, 288), (2528, 160)]
NV, NS = 1500, 384
Z = 344
F32, BF, I32, U16 = "float32", "bfloat16", "int32", "uint16"


def sb(n, d=F32):
    return ("sbuf", [128, n], d)


SCRATCH = {
    "bCI": sb(132, I32), "bC1": sb(132, I32), "bC2": sb(132, I32), "bC3": sb(132, I32), "bCPF": sb(132),
    "bC16": sb(128, U16), "bCP16": sb(132, U16),
    "bK8": sb(128, BF), "bK16": sb(128, BF), "bT8": sb(32, BF),
    "bJ": sb(128, BF), "bSB": sb(128, BF), "bYB": sb(128, BF), "bB": sb(128), "bB2": sb(128),
    "bSHW": sb(32), "bRX": sb(32), "bRN": sb(32), "bNLX": sb(32, U16), "bNLN": sb(32, U16), "bLM": sb(136),
    "bKEI": sb(8, BF), "bKEF": sb(128), "bKEB": sb(128, BF), "bON": sb(128, BF), "bMO": sb(128, BF), "bSTR": sb(E, BF),
    "bU": sb(M, BF), "bW": sb(M, BF), "bWG": sb(E), "bS": sb(E),
    "bG0": sb(E, BF), "bG": sb(E), "bV": sb(E + 16), "bWS": sb(512), "bW2": sb(M), "bX": sb(XW),
    "bSD0": sb(64), "bSD1": sb(64), "bSD2": sb(64), "bEW0": sb(80), "bEW1": sb(80), "bEW2": sb(80),
    "bQ0": ("dram", [N, 128, 8], F32), "bQ1": ("dram", [N, 128, 8], F32), "bQ2": ("dram", [N, 128, 8], F32),
    "bWT": sb(512), "bYG": sb(336),
    "bEI": sb(E), "bINV": sb(ME), "bISH": sb(ME), "bPOS": sb(ME), "bBS": sb(64), "bBE": sb(64),
    "bLSR": sb(512), "bDR": sb(512), "bNR": sb(512), "bLST": sb(32), "bDT": sb(32), "bNT": sb(32),
    "bLS16": sb(32, U16), "bD16": sb(32, U16), "bN16": sb(32, U16), "bIT": sb(MC), "bI16": sb(MC, U16),
    "bPT": sb(MC), "bPL": sb(22), "bPL16": sb(22, U16), "bE1": sb(E), "bE2": sb(E), "bCT": sb(128), "bCT16": sb(128, U16),
}
SCRATCH.update({"P%d" % k: ("psum", [128, 512], F32) for k in range(8)})
SEMAPHORES = ["kV", "kS", "kP", "kG", "loc", "arr0", "arr1", "arr2", "dconn", "dshare", "dke", "dw", "dw2", "dst", "du",
              "dish", "dew0", "dew1", "dew2", "dinv", "dls", "dd", "dn", "dct", "dpt", "dpl", "dy"]
A = AluOpType
AF = ActivationFunctionType


def rank_program(g, core, T, topo):
    rank = T.rank_of(core)
    if rank is None:
        return
    eng = {"V": g.vector, "S": g.scalar, "P": g.tensor, "G": g, "Y": g.sync}
    count, know, clock = {}, {q: {} for q in eng}, {}
    wr, rd = {}, {}

    def over(lst, a, b):
        return [e for e in lst if e[0] < b and a < e[1]]

    def need(q, r, w):
        own, out = "k" + q, {}
        for n, a, b in r:
            for e in over(wr.get(n, []), a, b):
                out[e[2]] = max(out.get(e[2], 0), e[3])
        for n, a, b in w:
            for e in over(wr.get(n, []), a, b):
                if not (e[2] == own and n[0] == "P"):
                    out[e[2]] = max(out.get(e[2], 0), e[3])
            for e in over(rd.get(n, []), a, b):
                if e[2] != own:
                    out[e[2]] = max(out.get(e[2], 0), e[3])
        return out

    def wait(q, deps):
        k = know[q]
        for s in sorted(deps, key=lambda s: -len(clock.get((s, deps[s]), {}))):
            v = deps[s]
            if k.get(s, 0) < v:
                eng[q].wait_ge(T.sem[s], v)
                for s2, v2 in clock.get((s, v), {}).items():
                    k[s2] = max(k.get(s2, 0), v2)
                k[s] = max(k.get(s, 0), v)

    def note(q, s, v, r, w):
        c = dict(know[q])
        c[s] = max(c.get(s, 0), v)
        clock[(s, v)] = c
        for n, a, b in w:
            wr[n] = [e for e in wr.get(n, []) if not (a <= e[0] and e[1] <= b)] + [(a, b, s, v)]
            rd[n] = [e for e in rd.get(n, []) if not (a <= e[0] and e[1] <= b)]
        for n, a, b in r:
            rd[n] = rd.get(n, []) + [(a, b, s, v)]

    def bank(regs):
        return [(n, 0, 512) if n[0] == "P" else (n, a, b) for n, a, b in regs]

    def op(q, fn, r, w):
        r, w = bank(r), bank(w)
        w = w + [x for x in r if x[0][0] == "P"]
        r2 = [x for x in r if not (x[0][0] == "P" and q == "P")]
        wait(q, need(q, r2, w))
        s = "k" + q
        count[s] = count.get(s, 0) + 1
        fn(eng[q]).then_inc(T.sem[s], 1)
        note(q, s, count[s], [x for x in r if x[0][0] != "P"], w)

    def dma(parts, s, r, w):
        qs = []
        for q, o, i in parts:
            if q not in qs:
                qs.append(q)
                wait(q, need(q, r, w))
            eng[q].dma_start(out=o, in_=i).then_inc(T.sem[s], 16)
            count[s] = count.get(s, 0) + 16
        note(qs[0], s, count[s], r, w)

    def gather(q, dst, a, n, win, wn, off, c0):
        o, i = T[dst][:, a:a + n], T[win][:, 0:wn].indirect(T[off][:, c0:c0 + n // 16])
        r = [(win, 0, wn), (off, c0, c0 + n // 16)]
        if q == "V":
            op("V", lambda e: e.tensor_copy(out=o, in_=i), r, [(dst, a, a + n)])
        else:
            op("S", lambda e: e.activation(out=o, in_=i, func=AF.Copy), r, [(dst, a, a + n)])

    def copy(q, dst, a, src, b, n, rows=128):
        o, i = T[dst][0:rows, a:a + n], T[src][0:rows, b:b + n]
        if q == "V":
            op("V", lambda e: e.tensor_copy(out=o, in_=i), [(src, b, b + n)], [(dst, a, a + n)])
        else:
            op("S", lambda e: e.activation(out=o, in_=i, func=AF.Copy), [(src, b, b + n)], [(dst, a, a + n)])

    def ts(dst, a, src, b, n, s1, op0):
        o, i = T[dst][:, a:a + n], T[src][:, b:b + n]
        op("V", lambda e: e.tensor_scalar(out=o, in0=i, scalar1=s1, scalar2=None, op0=op0), [(src, b, b + n)], [(dst, a, a + n)])

    def tt(dst, a, s0, b, s1, c, n, o):
        x, y, z = T[dst][:, a:a + n], T[s0][:, b:b + n], T[s1][:, c:c + n]
        op("V", lambda e: e.tensor_tensor(out=x, in0=y, in1=z, op=o), [(s0, b, b + n), (s1, c, c + n)], [(dst, a, a + n)])

    def fill(dst, a, n, val):
        op("V", lambda e: e.memset(T[dst][:, a:a + n], val), [], [(dst, a, a + n)])

    def mm(dst, a, n, lh, la, m, rh, ra, start=True, stop=True, rows=128):
        o, l, x = T[dst][0:m, a:a + n], T[lh][0:rows, la:la + m], T[rh][0:rows, ra:ra + n]
        op("P", lambda e: e.matmul(o, l, x, start, stop), [(lh, la, la + m), (rh, ra, ra + n)], [(dst, a, a + n)])

    def iota(dst, a, n, pat, base, cm):
        o = T[dst][:, a:a + n]
        op("G", lambda e: e.iota(o, pat, base, cm, allow_small_or_imprecise_dtypes=True), [], [(dst, a, a + n)])

    def select(dst, rows, a, n, pat, base=0):
        o, i = T[dst][0:rows, a:a + n], T.bON[0:rows, 0:n]
        op("G", lambda e: e.affine_select(o, i, pat, A.is_equal, 0.0, base, -1), [("bON", 0, n)], [(dst, a, a + n)])

    dma([("Y", T.bCI[:, 0:128], T.conn[:, :])], "dconn", [], [("bCI", 0, 128)])
    dma([("Y", T.bCI[:, 128:132], T.share[:, :])], "dshare", [], [("bCI", 128, 132)])
    dma([("Y", T.bW[k:k + 1, :], T.w[:, :]) for k in range(8)], "dw", [], [("bW", 0, M)])
    dma([("Y", T.bKEI[0:8, :], T.ke[:, :])], "dke", [], [("bKEI", 0, 8)])
    dma([("Y", T.bSTR[0:1, :], T.st[:, :])], "dst", [], [("bSTR", 0, E)])
    dma([("YS"[k % 2], T.bU[16 * k:16 * k + 16, :], T.u[:, :]) for k in range(8)], "du", [], [("bU", 0, M)])
    dma([("Y", T.bW[8 * k:8 * k + 8, :], T.bW[0:8, :]) for k in range(1, 16)], "dw2", [("bW", 0, M)], [("bW", 0, M)])
    fill("bON", 0, 128, 1.0)
    fill("bMO", 0, 128, -1.0)
    fill("bINV", 0, NV, float(E))
    iota("bEI", 0, 256, [[1, 256]], 0, 0)
    iota("bINV", NV + NS, ME - NV - NS, [[0, ME - NV - NS]], E, 0)
    select("bJ", 16, 0, 128, [[0, 8], [1, 16]])
    select("bSB", 8, 0, 128, [[1, 8], [0, 16]])
    select("bT8", 8, 0, 32, [[1, 8], [0, 4]])
    for k in range(4):
        select("bK8", 8, 32 * k, 32, [[4, 2], [0, 4], [1, 4]])
        select("bK16", 16, 32 * k, 32, [[0, 2], [4, 4], [0, 4]], k)
    iota("bV", E, 16, [[0, 16]], 0, 0)
    iota("bLM", 0, 136, [[0, 136]], 0, 0)
    iota("bISH", 0, Z, [[0, Z]], 64, 0)
    dma([("Y", T.bISH[:, Z * k:Z * k + Z], T.bISH[:, 0:Z]) for k in range(1, 8)], "dish", [("bISH", 0, Z)], [("bISH", Z, ME)])
    iota("bPOS", 0, ME, [[1, 16], [16, MC]], 0, 0)
    for h in range(2):
        iota("bBS", 32 * h, 32, [[256, 2], [64, 4], [2, 4]], h, 0)
        iota("bBE", 32 * h, 32, [[32, 2], [8, 4], [2, 4]], h, 0)
    iota("bEW0", 0, 80, [[0, 80]], 0, 0)
    for k in range(NS // 128):
        o = T.bINV[:, NV + 128 * k:NV + 128 * k + 128]
        op("S", lambda e: e.activation(out=o, in_=T.bON[:, 0:128], func=AF.Copy, scale=0.0, bias=float(E)),
           [("bON", 0, 128)], [("bINV", NV + 128 * k, NV + 128 * k + 128)])
    for n in (256, 512, 1024):
        o, i, b = T.bEI[:, n:2 * n], T.bEI[:, 0:n], float(n)
        op("S", lambda e: e.activation(out=o, in_=i, func=AF.Copy, bias=b), [("bEI", 0, n)], [("bEI", n, 2 * n)])
    ts("bC1", 0, "bCI", 0, 132, 15, A.bitwise_and)
    ts("bC2", 0, "bCI", 0, 132, 4, A.logical_shift_right)
    ts("bC3", 0, "bC1", 0, 132, float(MC), A.mult)
    copy("V", "bC16", 0, "bCI", 0, 128)
    tt("bCPF", 0, "bC3", 0, "bC2", 0, 132, A.add)
    copy("V", "bCP16", 0, "bCPF", 0, 132)
    for h in range(2):
        oi, ei = T.bINV[:, 0:ME].indirect(T.bCP16[:, 64 * h:64 * h + 64]), T.bEI[:, 1024 * h:1024 * h + 1024]
        op("V", lambda e: e.tensor_copy(out=oi, in_=ei), [("bEI", 1024 * h, 1024 * h + 1024), ("bCP16", 64 * h, 64 * h + 64)], [("bINV", 0, ME)])
    dma([("Y", T.bIT[:, :], T.bINV[0:128:16, :])], "dinv", [("bINV", 0, ME)], [("bIT", 0, MC)])
    for k in range(4):
        mm("P%d" % k, 0, 512, "bMO", 0, 128, "bSTR", 512 * k, rows=1)
    for k in (0, 1):
        gather("S", "bG0", 512 * k, 512, "bU", M, "bC16", 32 * k)
    mm("P7", 0, 128, "bJ", 0, 128, "bJ", 0, rows=16)
    copy("S", "bB", 0, "P7", 0, 128)
    mm("P6", 0, 128, "bKEI", 0, 8, "bSB", 0, rows=8)
    copy("S", "bYB", 0, "P6", 0, 128, rows=8)
    mm("P7", 0, 128, "bSB", 0, 128, "bYB", 0, rows=8)
    for a, b, n in ((0, 128, 4), (4, 128, 4)):
        copy("S", "bSHW", a, "bCPF", b, n)
    copy("S", "bSHW", 8, "bSHW", 0, 8)
    copy("S", "bSHW", 16, "bSHW", 0, 16)
    for k in (2, 3):
        gather("S", "bG0", 512 * k, 512, "bU", M, "bC16", 32 * k)
    mm("P4", 0, 128, "bK16", 0, 128, "bJ", 0, rows=16)
    copy("S", "bB2", 0, "P4", 0, 128)
    mm("P5", 0, 32, "bK8", 0, 128, "bT8", 0, rows=8)
    mm("P5", 32, 32, "bSB", 0, 128, "bT8", 0, rows=8)
    for k in range(4):
        gather("S", "bWG", 512 * k, 512, "bW", M, "bC16", 32 * k)
    tt("bRX", 0, "bSHW", 0, "P5", 0, 32, A.mult)
    mm("P6", 0, 32, "bB2", 0, 128, "bRX", 0)
    tt("bKEB", 0, "P7", 0, "bB", 0, 128, A.mult)
    tt("bRN", 0, "bSHW", 0, "P5", 32, 32, A.mult)
    copy("V", "bNLX", 0, "P6", 0, 32)
    mm("P6", 0, 32, "bB", 0, 128, "bRN", 0)
    gather("S", "bLSR", 0, 512, "bINV", ME, "bNLX", 0)
    dma([("Y", T.bLST[:, :], T.bLSR[0:128:16, :])], "dls", [("bLSR", 0, 512)], [("bLST", 0, 32)])
    for k in range(4):
        tt("bS", 512 * k, "bWG", 512 * k, "P%d" % k, 0, 512, A.mult)
        if k == 0:
            copy("V", "bNLN", 0, "P6", 0, 32)
    for k in range(4):
        mm("P%d" % (4 + k), 0, 512, "bKEB", 0, 128, "bG0", 512 * k)
    for k in range(4):
        tt("bV", 512 * k, "P%d" % (4 + k), 0, "bS", 512 * k, 512, A.mult)
    copy("V", "bLS16", 0, "bLST", 0, 32)
    op("S", lambda e: e.activation(out=T.bLM[:, 7:128:8], in_=T.bB[:, 0:16], func=AF.Copy), [("bB", 0, 16)], [("bLM", 0, 136)])
    gather("S", "bNR", 0, 512, "bPOS", ME, "bNLX", 0)
    dma([("Y", T.bNT[:, :], T.bNR[0:128:16, :])], "dn", [("bNR", 0, 512)], [("bNT", 0, 32)])
    copy("S", "bKEF", 0, "bKEB", 0, 128)

    others = [q for q in range(N) if q != rank]
    off = [q for q in others if topo.chip(T.cores[q]) != topo.chip(core)]
    on = [q for q in others if q not in off]
    eoff = topo.engines(core, T.cores[off[0]])
    eon = [e for e in topo.engines(core, T.cores[on[0]]) if e not in eoff]
    per = 2
    lanes = {q: eoff[per * k:per * k + per] for k, q in enumerate(off)}
    lanes.update({q: eon[per * k:per * k + per] for k, q in enumerate(on)})

    def send(t):
        copy("S", "bSD%d" % t, 0, "P3", 0, 64)
        wait("G", need("G", [("bSD%d" % t, 0, 64)], []))
        tr = []
        for q in off + on:
            rid, pid, _ = topo.addr(T.cores[q])
            tr.append(RemoteDMATransfer(dst_ids=[DstId(rid=rid, pnc=pid)], dma_engine_mask=sum(1 << e for e in lanes[q]),
                                        remote_sem=T.sem["arr%d" % t], src=T["bSD%d" % t][:, 8 * q:8 * q + 8],
                                        dst=T["bQ%d" % t][rank]))
        g.remote_dma_fused(tr, local_sem=T.sem["loc"])
        count["loc"] = count.get("loc", 0) + per * len(tr)
        s = "arr%d" % t
        count[s] = per * len(tr)
        for q in others:
            wr["bQ%d" % t] = wr.get("bQ%d" % t, []) + [(q, q + 1, s, count[s])]
        if t + 1 < R:
            iota("bEW%d" % (t + 1), 0, 80, [[0, 80]], 0, 0)

    def landed(t):
        dma([("Y", T["bEW%d" % t][16 * a:16 * b, 0:64], T["bQ%d" % t][a:b]) for a, b in ((0, rank), (rank + 1, N)) if a < b],
            "dew%d" % t, [("bQ%d" % t, 0, N)], [("bEW%d" % t, 0, 64)])

    def ngather(q, *ks):
        for k in ks:
            a, n = BLOCKS[k]
            gather(q, "bW2", a, n, "bV", E + 16, "bI16", a // 16)

    def node(k):
        a, n = BLOCKS[k]
        mm("P%d" % [4, 5, 7, 6][k % 4], 0, n, "bB", 0, 128, "bW2", a)

    def nadd(t, k):
        a, n = BLOCKS[k]
        tt("bX", a, "P%d" % [4, 5, 7, 6][k % 4], 0, "bX" if t else "bU", a, n, A.add)

    def shared(t):
        for h in range(4):
            x, y, z = T["bEW%d" % t][:, 0:80].indirect(T.bD16[:, 8 * h:8 * h + 8]), T.bWS[:, 128 * h:128 * h + 128], T.bWT[:, 128 * h:128 * h + 128]
            op("V", lambda e: e.tensor_tensor(out=z, in0=x, in1=y, op=A.add),
               [("bEW%d" % t, 0, 80), ("bD16", 8 * h, 8 * h + 8), ("bWS", 128 * h, 128 * h + 128)], [("bWT", 128 * h, 128 * h + 128)])

    def ssum():
        for h in range(4):
            mm("P%d" % h, 0, 128, "bB", 0, 128, "bWT", 128 * h)

    def sadd():
        for h in range(4):
            tt("bX", XS + 128 * h, "P%d" % h, 0, "bX", XS + 128 * h, 128, A.add)

    def permute(q, *js):
        for j in js:
            o, x = T.bE2[:, 128 * j:128 * j + 128], T.bE1[:, j:E:16]
            if q == "S":
                f = lambda e: e.activation(out=o, in_=x, func=AF.Copy)
            elif q == "V":
                f = lambda e: e.tensor_copy(out=o, in_=x)
            else:
                f = lambda e: e.affine_select(o, x, [[0, 128]], A.is_gt, 0.0, 1, 0)
            op(q, f, [("bE1", 0, E)], [("bE2", 128 * j, 128 * j + 128)])

    for t in range(R):
        if t:
            units = [(0, 64, "V"), (64, 64, "S"), (128, 128, "V"), (256, 256, "S"), (512, 256, "V"), (768, 256, "S"),
                     (1024, 256, "S"), (1280, 256, "S"), (1536, 256, "S"), (1792, 256, "S")]
            for a, n, q in units:
                gather(q, "bG", a, n, "bX", XW, "bCT16", a // 16)
            outs = [(0, 64), (64, 64), (128, 128)] + [(256 * k, 256) for k in range(1, 7)] + [(1792, 128), (1920, 64), (1984, 64)]
            for (a, n), b in zip(outs, [4, 5, 6, 7, 0, 1, 2, 3, 4, 5, 6, 7]):
                mm("P%d" % b, 0, n, "bKEF", 0, 128, "bG", a)
                tt("bV", a, "P%d" % b, 0, "bS", a, n, A.mult)
        for a, n in ((0, 64), (64, 64), (128, 128)):
            gather("S", "bWS", a, n, "bV", E + 16, "bLS16", a // 16)
            gather("V", "bWS", 256 + a, n, "bV", E + 16, "bLS16", 16 + a // 16)
        for s in (0, 4, 1, 5, 2, 6, 3, 7):
            mm("P3", 0, 64, "bLM", 7 - s, 128, "bWS", 64 * s, start=s == 0, stop=s == 7)
        if t == 0:
            send(t)
            copy("V", "bI16", 0, "bIT", 0, MC)
            for q in others:
                oq = T.bPOS[:, 0:ME].indirect(T.bNLN[:, 4 * q:4 * q + 4])
                op("V", lambda e: e.tensor_scalar(out=oq, in0=T.bBS[:, :], scalar1=1.0, scalar2=float(XS + 8 * q), op0=A.mult, op1=A.add),
                   [("bBS", 0, 64), ("bNLN", 4 * q, 4 * q + 4)], [("bPOS", 0, ME)])
            ngather("S", 2, 1)
            node(2)
            ngather("S", 0)
            node(0)
            oo = T.bISH[:, 0:ME].indirect(T.bCP16[:, 128:132])
            op("V", lambda e: e.tensor_copy(out=oo, in_=T.bBE[:, :]), [("bBE", 0, 64), ("bCP16", 128, 132)], [("bISH", 0, ME)])
            gather("S", "bE1", 0, 1024, "bPOS", ME, "bCP16", 0)
            gather("V", "bE1", 1024, 1024, "bPOS", ME, "bCP16", 64)
            node(1)
            gather("S", "bDR", 0, 512, "bISH", ME, "bNLX", 0)
            dma([("Y", T.bDT[:, :], T.bDR[0:128:16, :])], "dd", [("bDR", 0, 512)], [("bDT", 0, 32)])
            permute("V", 5)
            ngather("S", 3, 4)
            node(3)
            landed(t)
            permute("V", 1, 7, 3)
            permute("G", 6, 15, 10, 14)
            ngather("S", 5)
            nadd(t, 0)
            nadd(t, 1)
            permute("V", 2)
            permute("S", 4)
            node(4)
            nadd(t, 2)
            permute("V", 11)
            node(5)
            copy("V", "bD16", 0, "bDT", 0, 32)
            ts("bN16", 0, "bNT", 0, 32, float(M - 1), A.min)
            permute("G", 12, 13, 9, 0)
            shared(t)
            permute("S", 8)
            gather("S", "bX", XS, 512, "bU", M, "bN16", 0)
            ssum()
            ngather("S", 6)
            nadd(t, 4)
            nadd(t, 3)
            nadd(t, 5)
            node(6)
            sadd()
            dma([("Y", T.bCT[:, :], T.bE2[0:128:16, :])], "dct", [("bE2", 0, E)], [("bCT", 0, 128)])
            copy("V", "bCT16", 0, "bCT", 0, 128)
            nadd(t, 6)
            dma([("Y", T.bPT[:, :], T.bPOS[0:128:16, :])], "dpt", [("bPOS", 0, ME)], [("bPT", 0, MC)])
            dma([("Y", T.bPL[16 * k:16 * k + 16, 0:21], T.bPT[16 * k:16 * k + 16, 21 * k:21 * k + 21]) for k in range(8)],
                "dpl", [("bPT", 0, MC)], [("bPL", 0, 21)])
        else:
            ngather("S", 0)
            send(t)
            landed(t)
            ngather("V", 1)
            ngather("S", 2, 3, 4, 5, 6)
            for k in range(4):
                node(k)
                nadd(t, k)
            shared(t)
            node(4)
            node(5)
            nadd(t, 4)
            ssum()
            nadd(t, 5)
            node(6)
            sadd()
            nadd(t, 6)
        if t == 1:
            copy("V", "bPL16", 0, "bPL", 0, 21)
    gather("S", "bYG", 0, 160, "bX", XW, "bPL16", 0)
    gather("V", "bYG", 160, 176, "bX", XW, "bPL16", 10)
    dma([("YS"[k % 2], T.y[:, 336 * k:336 * k + 336], T.bYG[16 * k:16 * k + 16, :]) for k in range(8)], "dy", [("bYG", 0, 336)], [])
    for s in sorted(count):
        g.wait_ge(T.sem[s], count[s])
